import numpy as np
import ml_dtypes


def mxq(x, axis, fmt="e4m3"):
    dtype, down = {"e4m3": (ml_dtypes.float8_e4m3fn, 7), "e5m2": (ml_dtypes.float8_e5m2, 14)}[fmt]
    v = np.moveaxis(np.asarray(x, np.float32).astype(ml_dtypes.bfloat16).astype(np.float64), axis, -1)
    blocks = v.reshape(v.shape[:-1] + (-1, 32))
    amax = np.abs(blocks).max(-1, keepdims=True)
    byte = np.maximum(np.where(amax > 0, np.frexp(amax)[1] - 1 + 127, 0) - down, 1)
    scale = np.exp2(byte - 127.0)
    codes = (blocks / scale).astype(np.float32).astype(dtype).astype(np.float64)
    return np.moveaxis((codes * scale).reshape(v.shape), -1, axis)


WIDE = False


def mx_kscale(k):
    if not WIDE:
        return np.ones(k)
    levels = np.array([24, -24, 12, -12, 0])
    if k % 512:
        return np.exp2(np.random.permutation(np.resize(levels, k // 32))).repeat(32)
    a = np.empty((k // 512, 16))
    for p in range(k // 512):
        a[p, :8] = np.random.permutation(np.resize(levels, 8))
        for g in range(8):
            far = levels[np.abs(levels - a[p, g]) >= 10]
            a[p, g + 8] = far[np.random.randint(len(far))]
    return np.exp2(a.ravel()).repeat(32)


def f64(x):
    return np.asarray(x).astype(np.float64)


def striped(idx):
    return np.tile(idx.reshape(-1, 16).T, (8, 1)).astype(np.uint16)


def unstriped(offs):
    return offs[:16].T.reshape(-1).astype(np.int64)


E2M1 = np.array([0.0, 0.5, 1.0, 1.5, 2.0, 3.0, 4.0, 6.0, -0.0, -0.5, -1.0, -1.5, -2.0, -3.0, -4.0, -6.0])


def pack_weight(w, fmt):
    k, n = w.shape
    w = f64(np.asarray(w, np.float32).astype(ml_dtypes.bfloat16)).reshape(k // 32, 32, n)
    amax = np.abs(w).max(1)
    if fmt == "e4m3":
        byte = np.frexp(amax)[1] - 1 + 127 - 7
    else:
        mant, ex = np.frexp(amax / 6.0)
        byte = np.where(mant > 0.5, ex, ex - 1) + 127
    byte = np.clip(np.where(amax > 0, byte, 1), 1, 254)
    scaled = (w * np.exp2(127.0 - byte)[:, None, :]).reshape(k, n).astype(np.float32)
    by_word = np.ascontiguousarray(scaled.reshape(k // 512, 128, 4, n).transpose(0, 1, 3, 2))
    if fmt == "e4m3":
        words = by_word.astype(ml_dtypes.float8_e4m3fn).view(np.uint8)
    else:
        c = by_word.astype(ml_dtypes.float4_e2m1fn).view(np.uint8) & 0xF
        words = (c[..., 0::2] | (c[..., 1::2] << 4)).reshape(k // 512, 128, 2 * n)
    return np.ascontiguousarray(words), np.ascontiguousarray(byte.astype(np.uint8).reshape(k // 512, 16, n))


def unpack_weight(words, scales, fmt):
    g, _, n = scales.shape
    words = np.ascontiguousarray(words).reshape(g, 128, n, -1)
    if fmt == "e4m3":
        vals = words.view(ml_dtypes.float8_e4m3fn).astype(np.float64)
    else:
        nib = np.empty((g, 128, n, 4), np.uint8)
        nib[..., 0::2] = words & 0xF
        nib[..., 1::2] = words >> 4
        vals = E2M1[nib]
    vals = vals * np.repeat(np.exp2(scales.astype(np.float64) - 127.0), 8, axis=1)[..., None]
    return vals.transpose(0, 1, 3, 2).reshape(g * 512, n)


def pack_table4(v):
    words, scales = pack_weight(v, "e2m1")
    g, t = words.shape[0] // 2, v.shape[1]
    return np.ascontiguousarray(words.reshape(g, 2, 128, t, 2).transpose(0, 2, 3, 1, 4).reshape(g, 128, t, 4)), scales


def unpack_table4(words, scales):
    g, _, t, _ = words.shape
    return unpack_weight(words.reshape(g, 128, t, 2, 2).transpose(0, 3, 1, 2, 4).reshape(2 * g, 128, 2 * t), scales, "e2m1")


def silu(f):
    return f / (1.0 + np.exp(-np.maximum(f, -700.0)))


K, R, T, M, J = 1024, 512, 2048, 512, 512


def setup_inputs():
    n = np.random.standard_normal
    s = mx_kscale(K)[:, None]
    u = mx_kscale(R)[:, None]
    p_tab = pack_weight(n((K, T)) * s, "e4m3")
    p_tab2 = pack_table4(n((K, T)) * s)
    p_wb = pack_weight(n((K, R)) / np.sqrt(K) / s, "e2m1")
    return {
        "tab_words": p_tab[0],
        "tab_scales": p_tab[1],
        "tab2_words": p_tab2[0],
        "tab2_scales": p_tab2[1],
        "wa": (n((K, R)) / np.sqrt(K) / s).astype(np.float32),
        "wb_words": p_wb[0],
        "wb_scales": p_wb[1],
        "sa": (np.random.uniform(0.5, 2.0, R) * u[:, 0]).astype(np.float32),
        "sb": (np.random.uniform(0.5, 2.0, R) / u[:, 0]).astype(np.float32),
        "b": (0.3 * n(J)).astype(np.float32),
        "offs": striped(np.random.permutation(T)[:M]),
        "offs2": striped(np.random.permutation(T)[:J]),
    }


def reference(tab_words, tab_scales, tab2_words, tab2_scales, wa, wb_words, wb_scales, sa, sb, b, offs, offs2):
    idx = unstriped(offs)
    idx2 = unstriped(offs2)
    tab_ = unpack_weight(tab_words, tab_scales, "e4m3")[:, idx]
    tab2_ = unpack_table4(tab2_words, tab2_scales)[:, idx2]
    wa_ = mxq(f64(wa), 0, "e4m3")
    wb_ = unpack_weight(wb_words, wb_scales, "e2m1")
    za = wa_.T @ tab_
    zb = wb_.T @ tab2_
    ha = f64(sa)[:, None] * silu(za)
    hb = f64(sb)[:, None] * silu(zb)
    ha_ = mxq(ha, 0, "e4m3")
    hb_ = mxq(hb, 0, "e4m3")
    y = ha_.T @ hb_
    return y * 0.03125 + f64(b)[None, :]

@@ -1,0 +1,255 @@
+from contextlib import ExitStack
+
+import concourse.mybir as mybir
+from concourse.masks import make_identity
+
+K, R, T, M, J = 1024, 512, 2048, 512, 512
+FLOPS = 2 * K * R * M + 2 * K * R * J + 2 * R * M * J
+
+F32 = mybir.dt.float32
+BF16 = mybir.dt.bfloat16
+I32 = mybir.dt.int32
+U32 = mybir.dt.uint32
+U16 = mybir.dt.uint16
+U8 = mybir.dt.uint8
+FP8X4 = mybir.dt.float8_e4m3fn_x4
+FP4X4 = mybir.dt.float4_e2m1fn_x4
+MULT = mybir.AluOpType.mult
+ADD = mybir.AluOpType.add
+SILU = mybir.ActivationFunctionType.Silu
+
+P = 128
+PASSES = 2
+SLOTS = 4
+CHUNK = 128
+CHUNKS = 4
+HALF = 256
+TAB_ROW = (8, 12)
+
+
+def tile_list_biaff_silu_bias_kernel(
+    tc, tab_words, tab_scales, tab2_words, tab2_scales, wa, wb_words, wb_scales, sa, sb, b, offs, offs2, out
+):
+    nc = tc.nc
+    with ExitStack() as ctx:
+        keep = ctx.enter_context(tc.tile_pool(name="keep", bufs=1))
+        ring = ctx.enter_context(tc.tile_pool(name="ring", bufs=4))
+        zpool = ctx.enter_context(tc.psum_pool(name="zpool", bufs=4))
+        ypool = ctx.enter_context(tc.psum_pool(name="ypool", bufs=3))
+        spool = ctx.enter_context(tc.psum_pool(name="spool", bufs=1))
+
+        def held(name, shape, dtype):
+            return keep.tile(shape, dtype, name=name, align_bytes=64)
+
+        list_a = keep.tile([P, M // 16], U16, name="list_a")
+        list_b = keep.tile([P, J // 16], U16, name="list_b")
+        tab2_sc = keep.tile([P, T // 4], I32, name="tab2_sc", tag="stage0", align_bytes=64)
+        vb_sc1 = held("vb_sc1", [P, J // 4], I32)
+        tab_sc = held("tab_sc", [P, T // 4], I32)
+        wb_sc_raw = held("wb_sc_raw", [P, PASSES, R // 4], I32)
+        s_rows = held("s_rows", [P, P], F32)
+        warm = held("warm", [P, 1], F32)
+        ident = held("ident", [P, P], F32)
+        tab2_w = keep.tile([P, T], I32, name="tab2_w", tag="stage1", align_bytes=64)
+        wb_raw = keep.tile([P, PASSES, R // 2], I32, name="wb_raw", tag="stage2", align_bytes=64)
+        wa_raw = [held("wa_raw0", [P, SLOTS, R], F32)]
+        tab_w = []
+        b_col = held("b_col", [P, 4], F32)
+
+        nc.gpsimd.memset(tab2_sc[:], 0)
+        nc.vector.memset(wb_sc_raw[:], 0)
+        nc.vector.memset(s_rows[:], 0.0)
+        nc.vector.memset(tab_sc[:], 0)
+        nc.vector.memset(vb_sc1[:], 0)
+        nc.scalar.activation(warm[:], s_rows[:, 0:1], SILU)
+        make_identity(nc, ident[:])
+
+        def load_factor(row, vec):
+            nc.sync.dma_start(
+                s_rows[row : row + 4, :].rearrange("t (g i) -> t g i", i=8), vec.rearrange("(g t i) -> t g i", t=4, i=8)
+            )
+
+        def load_wa(a):
+            nc.sync.dma_start(wa_raw[a][:], wa[512 * a : 512 * (a + 1), :].rearrange("(p j) r -> p j r", j=4))
+
+        nc.sync.dma_start(list_b[:], offs2)
+        nc.sync.dma_start(list_a[:], offs)
+        nc.sync.dma_start(b_col[:], b.rearrange("(p c) -> p c", c=4))
+        t2s = tab2_scales.bitcast(I32)
+        for q in range(4):
+            nc.sync.dma_start(tab2_sc[32 * q : 32 * q + 8, :], t2s[:, 4 * q : 4 * q + 4, :])
+        nc.sync.dma_start(tab2_w[:], tab2_words[0].rearrange("p t i -> p (t i)").bitcast(I32))
+        wbs = wb_scales.bitcast(I32).rearrange("a (q r) n -> r q a n", r=4)
+        for r in range(4):
+            nc.sync.dma_start(wb_sc_raw[r:P:32, :, :], wbs[r])
+        load_factor(4, sb)
+        nc.sync.dma_start(wb_raw[:], wb_words.bitcast(I32).rearrange("a p n -> p a n"))
+        load_wa(0)
+        load_factor(0, sa)
+        ts = tab_scales.bitcast(I32)
+        for q in range(4):
+            nc.gpsimd.dma_start(tab_sc[32 * q + 8 : 32 * q + 16, :], ts[:, 4 * q : 4 * q + 4, :])
+
+        vb_sc0 = held("vb_sc0", [P, J], U8)
+        nc.vector.tensor_copy(vb_sc0[:], tab2_sc[:].bitcast(U8).indirect(list_b[:]))
+        nc.scalar.dma_start(vb_sc1[0 : P - 4, :], vb_sc0[4:P, :].bitcast(I32))
+        wa_raw.append(keep.tile([P, SLOTS, R], F32, name="wa_raw1", tag="stage0", align_bytes=64))
+        load_wa(1)
+        vb_sc = (vb_sc0[:], vb_sc1[:].bitcast(U8))
+        vb_pairs = held("vb_pairs", [P, J], U32)
+        nc.vector.tensor_copy(vb_pairs[:], tab2_w[:].bitcast(U32).indirect(list_b[:]))
+        wb_codes = held("wb_codes", [P, PASSES, R // 2], I32)
+        wb_sc = held("wb_sc", [P, PASSES, R // 4], I32)
+        for a in range(PASSES):
+            nc.vector.tensor_copy(
+                wb_codes[:, a, :].rearrange("p (t g w) -> p t g w", t=4, w=4),
+                wb_raw[:, a, :].rearrange("p (g t w) -> p t g w", t=4, w=4),
+            )
+        vb_codes = held("vb_codes", [P, PASSES, 2 * J], U8)
+        nc.vector.tensor_copy(
+            vb_codes[:].rearrange("p a n -> p (a n)").bitcast(U16).rearrange("p (a j) -> p a j", a=2),
+            vb_pairs[:].bitcast(U16).rearrange("p (j a) -> p a j", a=2),
+        )
+        for a in range(PASSES):
+            nc.vector.tensor_copy(
+                wb_sc[:, a, :].rearrange("p (t g w) -> p t g w", t=4, w=2),
+                wb_sc_raw[:, a, :].rearrange("p (g t w) -> p t g w", t=4, w=2),
+            )
+
+        for a in range(PASSES):
+            tab_w.append(keep.tile([P, T], I32, name="tab_w%d" % a, tag="stage%d" % (a + 1), align_bytes=64))
+            nc.sync.dma_start(tab_w[a][:], tab_words[a].rearrange("p t i -> p (t i)").bitcast(I32))
+
+        s_cols = spool.tile([P, P], F32, name="s_cols")
+        nc.tensor.transpose(s_cols[:], s_rows[:], ident[:])
+        b_bank = ypool.tile([P, 4, P], F32, name="y")
+        for c in range(4):
+            nc.tensor.transpose(b_bank[:, c, :], b_col[:, c : c + 1].to_broadcast([P, P]), ident[:])
+        b_all = held("b_all", [P, J], F32)
+        nc.scalar.copy(b_all[:].rearrange("p (n c) -> p n c", c=4), b_bank[:].rearrange("p c n -> p n c"))
+
+        def hidden_sums(c, w_codes, w_sc, v_codes, v_sc):
+            z = zpool.tile([P, SLOTS, CHUNK], F32, name="z")
+            for t in range(SLOTS):
+                for a in range(PASSES):
+                    nc.tensor.matmul_mx(
+                        z[:, t, :],
+                        lhsT=w_codes(a, t),
+                        lhsT_scale=w_sc(a, t),
+                        rhs=v_codes(a, c),
+                        rhs_scale=v_sc(a, c),
+                        start=(a == 0),
+                        stop=(a == PASSES - 1),
+                    )
+            act = ring.tile([P, CHUNK, SLOTS], F32, name="act")
+            nc.scalar.activation(act[:], z[:].rearrange("p t n -> p n t"), SILU)
+            return act
+
+        def scale_round(act, h, c, col):
+            nc.vector.tensor_tensor(
+                h[:, c * CHUNK : (c + 1) * CHUNK, :],
+                act[:],
+                s_cols[:, col : col + 4].unsqueeze(1).to_broadcast([P, CHUNK, SLOTS]),
+                MULT,
+            )
+
+        def quantize(h, codes, sc, lo, hi):
+            nc.vector.quantize_mx(
+                out=codes[:, lo:hi].bitcast(FP8X4), scales=sc[:, lo:hi], in_=h[:, lo:hi, :].rearrange("p n t -> p (n t)")
+            )
+
+        wa_bf = [held("wa_bf%d" % a, [P, R, SLOTS], BF16) for a in range(PASSES)]
+
+        def cast_wa(a, t, copy):
+            src = wa_raw[a][:].rearrange("p j (g t i) -> p t g i j", t=4, i=8)
+            dst = wa_bf[a][:].rearrange("p (t g i) j -> p t g i j", t=4, i=8)
+            copy(dst[:, t], src[:, t])
+
+        cast_wa(0, 0, nc.scalar.copy)
+        cast_wa(0, 2, nc.vector.tensor_copy)
+        cast_wa(0, 3, nc.vector.tensor_copy)
+
+        hb = held("hb", [P, J, SLOTS], BF16)
+        hb_codes = held("hb_codes", [P, J], U32)
+        hb_sc = held("hb_sc", [P, J], U8)
+        acts_b = []
+        for c in range(CHUNKS):
+            acts_b.append(
+                hidden_sums(
+                    c,
+                    lambda a, t: wb_codes[:, a, 64 * t : 64 * (t + 1)].bitcast(FP4X4),
+                    lambda a, t: wb_sc[:, a, 32 * t : 32 * (t + 1)].bitcast(U8),
+                    lambda a, c: vb_codes[:, a, 2 * CHUNK * c : 2 * CHUNK * (c + 1)].bitcast(FP4X4),
+                    lambda a, c: vb_sc[a][:, CHUNK * c : CHUNK * (c + 1)],
+                )
+            )
+
+        va_sc = held("va_sc", [P, M], U8)
+        wa_codes = [held("wa_codes%d" % a, [P, R], U32) for a in range(PASSES)]
+        wa_sc = [held("wa_sc%d" % a, [P, R], U8) for a in range(PASSES)]
+
+        for c in range(CHUNKS):
+            scale_round(acts_b[c], hb, c, 4)
+        nc.vector.tensor_copy(va_sc[:], tab_sc[:].bitcast(U8).indirect(list_a[:]))
+        cast_wa(0, 1, nc.scalar.copy)
+        for t in range(SLOTS):
+            cast_wa(1, t, nc.scalar.copy)
+        va_codes = [held("va_codes%d" % a, [P, M], U32) for a in range(PASSES)]
+
+        def gather_a(a, h):
+            nc.vector.tensor_copy(
+                va_codes[a][:, h * HALF : (h + 1) * HALF],
+                tab_w[a][:].bitcast(U32).indirect(list_a[:, 16 * h : 16 * (h + 1)]),
+            )
+
+        quantize(hb, hb_codes, hb_sc, 0, J)
+        quantize(wa_bf[0], wa_codes[0], wa_sc[0], 0, R)
+        gather_a(0, 0)
+        gather_a(0, 1)
+        quantize(wa_bf[1], wa_codes[1], wa_sc[1], 0, R)
+        gather_a(1, 0)
+        gather_a(1, 1)
+
+        ha = held("ha", [P, M, SLOTS], BF16)
+        ha_codes = held("ha_codes", [P, M], U32)
+        ha_sc = held("ha_sc", [P, M], U8)
+        acts_a = []
+        for c in range(CHUNKS):
+            acts_a.append(
+                hidden_sums(
+                    c,
+                    lambda a, t: wa_codes[a][:, P * t : P * (t + 1)].bitcast(FP8X4),
+                    lambda a, t: wa_sc[a][:, P * t : P * (t + 1)],
+                    lambda a, c: va_codes[a][:, CHUNK * c : CHUNK * (c + 1)].bitcast(FP8X4),
+                    lambda a, c: va_sc[TAB_ROW[a] : P, CHUNK * c : CHUNK * (c + 1)],
+                )
+            )
+
+        def score(c):
+            cols = slice(c * CHUNK, (c + 1) * CHUNK)
+            y = ypool.tile([P, J], F32, name="y")
+            nc.tensor.matmul_mx(
+                y[:],
+                lhsT=ha_codes[:, cols].bitcast(FP8X4),
+                lhsT_scale=ha_sc[:, cols],
+                rhs=hb_codes[:].bitcast(FP8X4),
+                rhs_scale=hb_sc[:],
+                start=True,
+                stop=True,
+            )
+            return y
+
+        def finish(c, y):
+            res = ring.tile([P, J], F32, name="res")
+            nc.vector.scalar_tensor_tensor(res[:], y[:], 0.03125, b_all[:], MULT, ADD)
+            nc.sync.dma_start(out[c * CHUNK : (c + 1) * CHUNK, :], res[:])
+
+        ys = {}
+        for step in range(CHUNKS + 3):
+            if step < CHUNKS:
+                scale_round(acts_a[step], ha, step, 0)
+            if 0 <= step - 1 < CHUNKS:
+                quantize(ha, ha_codes, ha_sc, (step - 1) * CHUNK, step * CHUNK)
+                ys[step - 1] = score(step - 1)
+            if 0 <= step - 3 < CHUNKS:
+                finish(step - 3, ys[step - 3])

@@ -34,35 +34,35 @@ def tile_list_biaff_silu_bias_kernel(
     with ExitStack() as ctx:
         keep = ctx.enter_context(tc.tile_pool(name="keep", bufs=1))
         ring = ctx.enter_context(tc.tile_pool(name="ring", bufs=4))
-        zpool = ctx.enter_context(tc.psum_pool(name="zpool", bufs=4))
-        ypool = ctx.enter_context(tc.psum_pool(name="ypool", bufs=3))
-        spool = ctx.enter_context(tc.psum_pool(name="spool", bufs=1))
+        psum = ctx.enter_context(tc.psum_pool(name="psum", bufs=8))
 
-        def held(name, shape, dtype):
-            return keep.tile(shape, dtype, name=name, align_bytes=64)
+        def bank():
+            return psum.tile([P, 512], F32, name="bank")
+
+        def held(name, shape, dtype, slot=None):
+            return keep.tile(shape, dtype, name=name, tag=slot or name, align_bytes=64)
 
         list_a = keep.tile([P, M // 16], U16, name="list_a")
         list_b = keep.tile([P, J // 16], U16, name="list_b")
-        tab2_sc = keep.tile([P, T // 4], I32, name="tab2_sc", tag="stage0", align_bytes=64)
-        vb_sc1 = held("vb_sc1", [P, J // 4], I32)
+        tab2_sc = [held("tab2_sc%d" % a, [P, T // 4], I32) for a in range(PASSES)]
         tab_sc = held("tab_sc", [P, T // 4], I32)
         wb_sc_raw = held("wb_sc_raw", [P, PASSES, R // 4], I32)
         s_rows = held("s_rows", [P, P], F32)
         warm = held("warm", [P, 1], F32)
         ident = held("ident", [P, P], F32)
-        tab2_w = keep.tile([P, T], I32, name="tab2_w", tag="stage1", align_bytes=64)
-        wb_raw = keep.tile([P, PASSES, R // 2], I32, name="wb_raw", tag="stage2", align_bytes=64)
-        wa_raw = [held("wa_raw0", [P, SLOTS, R], F32)]
-        tab_w = []
+        tab2_w = held("tab2_w", [P, T], I32)
+        wb_raw = held("wb_raw", [P, PASSES, R // 2], I32)
+        wa_raw = [held("wa_raw%d" % a, [P, SLOTS, R], F32) for a in range(PASSES)]
+        tab_w = [held("tab_w%d" % a, [P, T], I32) for a in range(PASSES)]
         b_col = held("b_col", [P, 4], F32)
 
-        nc.gpsimd.memset(tab2_sc[:], 0)
+        nc.gpsimd.memset(tab2_sc[0][:], 0)
+        nc.vector.memset(tab2_sc[1][:], 0)
         nc.vector.memset(wb_sc_raw[:], 0)
         nc.vector.memset(s_rows[:], 0.0)
         nc.vector.memset(tab_sc[:], 0)
-        nc.vector.memset(vb_sc1[:], 0)
-        nc.scalar.activation(warm[:], s_rows[:, 0:1], SILU)
         make_identity(nc, ident[:])
+        nc.scalar.activation(warm[:], ident[:, 0:1], SILU)
 
         def load_factor(row, vec):
             nc.sync.dma_start(
@@ -72,84 +72,71 @@ def tile_list_biaff_silu_bias_kernel(
         def load_wa(a):
             nc.sync.dma_start(wa_raw[a][:], wa[512 * a : 512 * (a + 1), :].rearrange("(p j) r -> p j r", j=4))
 
+        def load_tab(a):
+            nc.sync.dma_start(tab_w[a][:], tab_words[a].rearrange("p t i -> p (t i)").bitcast(I32))
+
         nc.sync.dma_start(list_b[:], offs2)
         nc.sync.dma_start(list_a[:], offs)
         nc.sync.dma_start(b_col[:], b.rearrange("(p c) -> p c", c=4))
-        t2s = tab2_scales.bitcast(I32)
-        for q in range(4):
-            nc.sync.dma_start(tab2_sc[32 * q : 32 * q + 8, :], t2s[:, 4 * q : 4 * q + 4, :])
-        nc.sync.dma_start(tab2_w[:], tab2_words[0].rearrange("p t i -> p (t i)").bitcast(I32))
-        wbs = wb_scales.bitcast(I32).rearrange("a (q r) n -> r q a n", r=4)
+        t2s = tab2_scales.bitcast(I32).rearrange("a (q r) n -> a r q n", r=4)
         for r in range(4):
-            nc.sync.dma_start(wb_sc_raw[r:P:32, :, :], wbs[r])
-        load_factor(4, sb)
+            nc.sync.dma_start(tab2_sc[0][r:P:32, :], t2s[0, r])
+        nc.sync.dma_start(tab2_w[:], tab2_words[0].rearrange("p t i -> p (t i)").bitcast(I32))
+        for r in range(4):
+            nc.sync.dma_start(tab2_sc[1][r:P:32, :], t2s[1, r])
         nc.sync.dma_start(wb_raw[:], wb_words.bitcast(I32).rearrange("a p n -> p a n"))
+        wbs = wb_scales.bitcast(I32).rearrange("a (q r) n -> r q a n", r=4)
+        nc.sync.dma_start(wb_sc_raw[0:P:32, :, :], wbs[0])
         load_wa(0)
-        load_factor(0, sa)
+        for r in range(1, 4):
+            nc.sync.dma_start(wb_sc_raw[r:P:32, :, :], wbs[r])
         ts = tab_scales.bitcast(I32)
         for q in range(4):
-            nc.gpsimd.dma_start(tab_sc[32 * q + 8 : 32 * q + 16, :], ts[:, 4 * q : 4 * q + 4, :])
-
-        vb_sc0 = held("vb_sc0", [P, J], U8)
-        nc.vector.tensor_copy(vb_sc0[:], tab2_sc[:].bitcast(U8).indirect(list_b[:]))
-        nc.scalar.dma_start(vb_sc1[0 : P - 4, :], vb_sc0[4:P, :].bitcast(I32))
-        wa_raw.append(keep.tile([P, SLOTS, R], F32, name="wa_raw1", tag="stage0", align_bytes=64))
+            nc.sync.dma_start(tab_sc[32 * q + 8 : 32 * q + 16, :], ts[:, 4 * q : 4 * q + 4, :])
+        load_tab(0)
+        load_factor(4, sb)
+        load_factor(0, sa)
         load_wa(1)
-        vb_sc = (vb_sc0[:], vb_sc1[:].bitcast(U8))
+        load_tab(1)
+
+        vb_sc_all = held("vb_sc_all", [P, PASSES, J], U8)
+        nc.vector.tensor_copy(vb_sc_all[:, 0, :], tab2_sc[0][:].bitcast(U8).indirect(list_b[:]))
+        vb_sc = (vb_sc_all[:, 0, :], vb_sc_all[:, 1, :])
         vb_pairs = held("vb_pairs", [P, J], U32)
         nc.vector.tensor_copy(vb_pairs[:], tab2_w[:].bitcast(U32).indirect(list_b[:]))
-        wb_codes = held("wb_codes", [P, PASSES, R // 2], I32)
-        wb_sc = held("wb_sc", [P, PASSES, R // 4], I32)
-        for a in range(PASSES):
-            nc.vector.tensor_copy(
-                wb_codes[:, a, :].rearrange("p (t g w) -> p t g w", t=4, w=4),
-                wb_raw[:, a, :].rearrange("p (g t w) -> p t g w", t=4, w=4),
-            )
         vb_codes = held("vb_codes", [P, PASSES, 2 * J], U8)
+        nc.vector.tensor_copy(vb_sc_all[:, 1, :], tab2_sc[1][:].bitcast(U8).indirect(list_b[:]))
         nc.vector.tensor_copy(
             vb_codes[:].rearrange("p a n -> p (a n)").bitcast(U16).rearrange("p (a j) -> p a j", a=2),
             vb_pairs[:].bitcast(U16).rearrange("p (j a) -> p a j", a=2),
         )
-        for a in range(PASSES):
-            nc.vector.tensor_copy(
-                wb_sc[:, a, :].rearrange("p (t g w) -> p t g w", t=4, w=2),
-                wb_sc_raw[:, a, :].rearrange("p (g t w) -> p t g w", t=4, w=2),
-            )
+        wb_codes = held("wb_codes", [P, PASSES, R // 2], I32)
+        wb_sc = held("wb_sc", [P, PASSES, R // 4], I32)
+        nc.vector.tensor_copy(
+            wb_codes[:].rearrange("p a (t g w) -> p a t g w", t=4, w=4),
+            wb_raw[:].rearrange("p a (g t w) -> p a t g w", t=4, w=4),
+        )
+        nc.vector.tensor_copy(
+            wb_sc[:].rearrange("p a (t g w) -> p a t g w", t=4, w=2),
+            wb_sc_raw[:].rearrange("p a (g t w) -> p a t g w", t=4, w=2),
+        )
 
-        for a in range(PASSES):
-            tab_w.append(keep.tile([P, T], I32, name="tab_w%d" % a, tag="stage%d" % (a + 1), align_bytes=64))
-            nc.sync.dma_start(tab_w[a][:], tab_words[a].rearrange("p t i -> p (t i)").bitcast(I32))
-
-        s_cols = spool.tile([P, P], F32, name="s_cols")
-        nc.tensor.transpose(s_cols[:], s_rows[:], ident[:])
-        b_bank = ypool.tile([P, 4, P], F32, name="y")
+        b_bank = bank()
         for c in range(4):
-            nc.tensor.transpose(b_bank[:, c, :], b_col[:, c : c + 1].to_broadcast([P, P]), ident[:])
+            nc.tensor.transpose(b_bank[:, c * P : (c + 1) * P], b_col[:, c : c + 1].to_broadcast([P, P]), ident[:])
         b_all = held("b_all", [P, J], F32)
-        nc.scalar.copy(b_all[:].rearrange("p (n c) -> p n c", c=4), b_bank[:].rearrange("p c n -> p n c"))
+        nc.scalar.copy(b_all[:].rearrange("p (n c) -> p n c", c=4), b_bank[:].rearrange("p (c n) -> p n c", c=4))
 
-        def hidden_sums(c, w_codes, w_sc, v_codes, v_sc):
-            z = zpool.tile([P, SLOTS, CHUNK], F32, name="z")
-            for t in range(SLOTS):
-                for a in range(PASSES):
-                    nc.tensor.matmul_mx(
-                        z[:, t, :],
-                        lhsT=w_codes(a, t),
-                        lhsT_scale=w_sc(a, t),
-                        rhs=v_codes(a, c),
-                        rhs_scale=v_sc(a, c),
-                        start=(a == 0),
-                        stop=(a == PASSES - 1),
-                    )
-            act = ring.tile([P, CHUNK, SLOTS], F32, name="act")
-            nc.scalar.activation(act[:], z[:].rearrange("p t n -> p n t"), SILU)
-            return act
+        s_cols = held("s_cols", [P, 2 * SLOTS], F32)
+        sa_cols = s_cols[:, 0:SLOTS]
+        sb_cols = s_cols[:, SLOTS : 2 * SLOTS]
 
-        def scale_round(act, h, c, col):
+        def scale_round(act, h, lo, hi, s_cols):
+            groups = (hi - lo) // 4
             nc.vector.tensor_tensor(
-                h[:, c * CHUNK : (c + 1) * CHUNK, :],
-                act[:],
-                s_cols[:, col : col + 4].unsqueeze(1).to_broadcast([P, CHUNK, SLOTS]),
+                h[:, lo:hi, :].rearrange("p (c i) t -> p c t i", i=4),
+                act[:, :, lo:hi].rearrange("p t (c i) -> p c t i", i=4),
+                s_cols.unsqueeze(1).unsqueeze(3).to_broadcast([P, groups, SLOTS, 4]),
                 MULT,
             )
 
@@ -158,43 +145,51 @@ def tile_list_biaff_silu_bias_kernel(
                 out=codes[:, lo:hi].bitcast(FP8X4), scales=sc[:, lo:hi], in_=h[:, lo:hi, :].rearrange("p n t -> p (n t)")
             )
 
-        wa_bf = [held("wa_bf%d" % a, [P, R, SLOTS], BF16) for a in range(PASSES)]
+        wa_bf = [held("wa_bf0", [P, R, SLOTS], BF16)]
 
         def cast_wa(a, t, copy):
-            src = wa_raw[a][:].rearrange("p j (g t i) -> p t g i j", t=4, i=8)
-            dst = wa_bf[a][:].rearrange("p (t g i) j -> p t g i j", t=4, i=8)
+            src = wa_raw[a][:].rearrange("p j (g t u i) -> p t g u j i", t=4, u=2, i=4)
+            dst = wa_bf[a][:].rearrange("p (t g u i) j -> p t g u j i", t=4, u=2, i=4)
             copy(dst[:, t], src[:, t])
 
-        cast_wa(0, 0, nc.scalar.copy)
-        cast_wa(0, 2, nc.vector.tensor_copy)
-        cast_wa(0, 3, nc.vector.tensor_copy)
+
+        for t in range(SLOTS):
+            cast_wa(0, t, nc.scalar.copy)
 
         hb = held("hb", [P, J, SLOTS], BF16)
         hb_codes = held("hb_codes", [P, J], U32)
         hb_sc = held("hb_sc", [P, J], U8)
-        acts_b = []
-        for c in range(CHUNKS):
-            acts_b.append(
-                hidden_sums(
-                    c,
-                    lambda a, t: wb_codes[:, a, 64 * t : 64 * (t + 1)].bitcast(FP4X4),
-                    lambda a, t: wb_sc[:, a, 32 * t : 32 * (t + 1)].bitcast(U8),
-                    lambda a, c: vb_codes[:, a, 2 * CHUNK * c : 2 * CHUNK * (c + 1)].bitcast(FP4X4),
-                    lambda a, c: vb_sc[a][:, CHUNK * c : CHUNK * (c + 1)],
-                )
-            )
+        act_b = held("act_b", [P, 2, J, 2], F32)
+        for h in range(2):
+            cols = slice(h * HALF, (h + 1) * HALF)
+            for t in range(SLOTS):
+                if t % 2 == 0:
+                    z = bank()
+                zt = z[:, (t % 2) * HALF : (t % 2 + 1) * HALF]
+                for a in range(PASSES):
+                    nc.tensor.matmul_mx(
+                        zt,
+                        lhsT=wb_codes[:, a, 64 * t : 64 * (t + 1)].bitcast(FP4X4),
+                        lhsT_scale=wb_sc[:, a, 32 * t : 32 * (t + 1)].bitcast(U8),
+                        rhs=vb_codes[:, a, 2 * HALF * h : 2 * HALF * (h + 1)].bitcast(FP4X4),
+                        rhs_scale=vb_sc[a][:, cols],
+                        start=(a == 0),
+                        stop=(a == PASSES - 1),
+                    )
+                if t % 2 == 1:
+                    nc.scalar.activation(act_b[:, t // 2, cols, :], z[:].rearrange("p (e n) -> p n e", e=2), SILU)
+            if h == 0:
+                s_bank = bank()
+                nc.tensor.transpose(s_bank[:, 0:P], s_rows[:], ident[:])
+                nc.vector.tensor_copy(s_cols[:], s_bank[:, 0 : 2 * SLOTS])
 
-        va_sc = held("va_sc", [P, M], U8)
-        wa_codes = [held("wa_codes%d" % a, [P, R], U32) for a in range(PASSES)]
+        va_sc = held("va_sc", [P, M], U8, "wb_sc_raw")
+        nc.vector.tensor_copy(va_sc[:], tab_sc[:].bitcast(U8).indirect(list_a[:]))
+        wa_codes = [held("wa_codes0", [P, R], U32, "tab_sc"), held("wa_codes1", [P, R], U32)]
         wa_sc = [held("wa_sc%d" % a, [P, R], U8) for a in range(PASSES)]
 
-        for c in range(CHUNKS):
-            scale_round(acts_b[c], hb, c, 4)
-        nc.vector.tensor_copy(va_sc[:], tab_sc[:].bitcast(U8).indirect(list_a[:]))
-        cast_wa(0, 1, nc.scalar.copy)
-        for t in range(SLOTS):
-            cast_wa(1, t, nc.scalar.copy)
-        va_codes = [held("va_codes%d" % a, [P, M], U32) for a in range(PASSES)]
+        quantize(wa_bf[0], wa_codes[0], wa_sc[0], 0, R)
+        va_codes = [held("va_codes0", [P, M], U32, "wa_bf0")]
 
         def gather_a(a, h):
             nc.vector.tensor_copy(
@@ -202,32 +197,54 @@ def tile_list_biaff_silu_bias_kernel(
                 tab_w[a][:].bitcast(U32).indirect(list_a[:, 16 * h : 16 * (h + 1)]),
             )
 
+        def sums_a(z, a, h, t):
+            cols = slice(h * HALF, (h + 1) * HALF)
+            nc.tensor.matmul_mx(
+                z[:, 0:HALF],
+                lhsT=wa_codes[a][:, P * t : P * (t + 1)].bitcast(FP8X4),
+                lhsT_scale=wa_sc[a][:, P * t : P * (t + 1)],
+                rhs=va_codes[a][:, cols].bitcast(FP8X4),
+                rhs_scale=va_sc[TAB_ROW[a] : P, cols],
+                start=(a == 0),
+                stop=(a == PASSES - 1),
+            )
+
+        za = {}
+        nc.vector.tensor_copy(va_codes[0][:], tab_w[0][:].bitcast(U32).indirect(list_a[:]))
+        for h in range(2):
+            for t in range(SLOTS):
+                za[h, t] = bank()
+                sums_a(za[h, t], 0, h, t)
+        for h in range(2):
+            cols = slice(h * HALF, (h + 1) * HALF)
+            nc.vector.tensor_tensor(
+                hb[:, cols, :].rearrange("p n (u e) -> p n u e", e=2),
+                act_b[:, :, cols, :].rearrange("p u n e -> p n u e"),
+                sb_cols.rearrange("p (u e) -> p u e", e=2).unsqueeze(1).to_broadcast([P, HALF, 2, 2]),
+                MULT,
+            )
         quantize(hb, hb_codes, hb_sc, 0, J)
-        quantize(wa_bf[0], wa_codes[0], wa_sc[0], 0, R)
-        gather_a(0, 0)
-        gather_a(0, 1)
-        quantize(wa_bf[1], wa_codes[1], wa_sc[1], 0, R)
+        va_codes.append(held("va_codes1", [P, M], U32, "hb"))
+        wa_bf.append(held("wa_bf1", [P, R, SLOTS], BF16, "vb_codes"))
+        for t in range(SLOTS):
+            cast_wa(1, t, nc.scalar.copy)
         gather_a(1, 0)
+        quantize(wa_bf[1], wa_codes[1], wa_sc[1], 0, HALF)
         gather_a(1, 1)
+        quantize(wa_bf[1], wa_codes[1], wa_sc[1], HALF, R)
+        act_a = held("act_a", [P, SLOTS, M], F32)
+        for h in range(2):
+            for t in range(SLOTS):
+                sums_a(za[h, t], 1, h, t)
+                nc.scalar.activation(act_a[:, t, h * HALF : (h + 1) * HALF], za[h, t][:, 0:HALF], SILU)
 
         ha = held("ha", [P, M, SLOTS], BF16)
         ha_codes = held("ha_codes", [P, M], U32)
         ha_sc = held("ha_sc", [P, M], U8)
-        acts_a = []
-        for c in range(CHUNKS):
-            acts_a.append(
-                hidden_sums(
-                    c,
-                    lambda a, t: wa_codes[a][:, P * t : P * (t + 1)].bitcast(FP8X4),
-                    lambda a, t: wa_sc[a][:, P * t : P * (t + 1)],
-                    lambda a, c: va_codes[a][:, CHUNK * c : CHUNK * (c + 1)].bitcast(FP8X4),
-                    lambda a, c: va_sc[TAB_ROW[a] : P, CHUNK * c : CHUNK * (c + 1)],
-                )
-            )
 
         def score(c):
             cols = slice(c * CHUNK, (c + 1) * CHUNK)
-            y = ypool.tile([P, J], F32, name="y")
+            y = bank()
             nc.tensor.matmul_mx(
                 y[:],
                 lhsT=ha_codes[:, cols].bitcast(FP8X4),
@@ -247,7 +264,7 @@ def tile_list_biaff_silu_bias_kernel(
         ys = {}
         for step in range(CHUNKS + 3):
             if step < CHUNKS:
-                scale_round(acts_a[step], ha, step, 0)
+                scale_round(act_a, ha, step * CHUNK, (step + 1) * CHUNK, sa_cols)
             if 0 <= step - 1 < CHUNKS:
                 quantize(ha, ha_codes, ha_sc, (step - 1) * CHUNK, step * CHUNK)
                 ys[step - 1] = score(step - 1)

@@ -19,12 +19,13 @@ ADD = mybir.AluOpType.add
 SILU = mybir.ActivationFunctionType.Silu
 
 P = 128
-PASSES = 2
+PASSES = K // 512
 SLOTS = 4
 CHUNK = 128
-CHUNKS = 4
+CHUNKS = M // CHUNK
 HALF = 256
 TAB_ROW = (8, 12)
+FINISH_LAG = 3
 
 
 def tile_list_biaff_silu_bias_kernel(
@@ -33,7 +34,7 @@ def tile_list_biaff_silu_bias_kernel(
     nc = tc.nc
     with ExitStack() as ctx:
         keep = ctx.enter_context(tc.tile_pool(name="keep", bufs=1))
-        ring = ctx.enter_context(tc.tile_pool(name="ring", bufs=4))
+        ring = ctx.enter_context(tc.tile_pool(name="ring", bufs=CHUNKS))
         psum = ctx.enter_context(tc.psum_pool(name="psum", bufs=8))
 
         def bank():
@@ -92,20 +93,19 @@ def tile_list_biaff_silu_bias_kernel(
             nc.sync.dma_start(wb_sc_raw[r:P:32, :, :], wbs[r])
         ts = tab_scales.bitcast(I32)
         for q in range(4):
-            nc.sync.dma_start(tab_sc[32 * q + 8 : 32 * q + 16, :], ts[:, 4 * q : 4 * q + 4, :])
+            nc.sync.dma_start(tab_sc[32 * q + TAB_ROW[0] : 32 * q + TAB_ROW[1] + 4, :], ts[:, 4 * q : 4 * q + 4, :])
         load_tab(0)
-        load_factor(4, sb)
+        load_factor(SLOTS, sb)
         load_factor(0, sa)
         load_wa(1)
         load_tab(1)
 
-        vb_sc_all = held("vb_sc_all", [P, PASSES, J], U8)
-        nc.vector.tensor_copy(vb_sc_all[:, 0, :], tab2_sc[0][:].bitcast(U8).indirect(list_b[:]))
-        vb_sc = (vb_sc_all[:, 0, :], vb_sc_all[:, 1, :])
+        vb_sc = held("vb_sc_all", [P, PASSES, J], U8)
+        nc.vector.tensor_copy(vb_sc[:, 0, :], tab2_sc[0][:].bitcast(U8).indirect(list_b[:]))
         vb_pairs = held("vb_pairs", [P, J], U32)
         nc.vector.tensor_copy(vb_pairs[:], tab2_w[:].bitcast(U32).indirect(list_b[:]))
         vb_codes = held("vb_codes", [P, PASSES, 2 * J], U8)
-        nc.vector.tensor_copy(vb_sc_all[:, 1, :], tab2_sc[1][:].bitcast(U8).indirect(list_b[:]))
+        nc.vector.tensor_copy(vb_sc[:, 1, :], tab2_sc[1][:].bitcast(U8).indirect(list_b[:]))
         nc.vector.tensor_copy(
             vb_codes[:].rearrange("p a n -> p (a n)").bitcast(U16).rearrange("p (a j) -> p a j", a=2),
             vb_pairs[:].bitcast(U16).rearrange("p (j a) -> p a j", a=2),
@@ -131,30 +131,22 @@ def tile_list_biaff_silu_bias_kernel(
         sa_cols = s_cols[:, 0:SLOTS]
         sb_cols = s_cols[:, SLOTS : 2 * SLOTS]
 
-        def scale_round(act, h, lo, hi, s_cols):
-            groups = (hi - lo) // 4
-            nc.vector.tensor_tensor(
-                h[:, lo:hi, :].rearrange("p (c i) t -> p c t i", i=4),
-                act[:, :, lo:hi].rearrange("p t (c i) -> p c t i", i=4),
-                s_cols.unsqueeze(1).unsqueeze(3).to_broadcast([P, groups, SLOTS, 4]),
-                MULT,
-            )
-
-        def quantize(h, codes, sc, lo, hi):
+        def quantize(values, codes, scales, lo, hi):
             nc.vector.quantize_mx(
-                out=codes[:, lo:hi].bitcast(FP8X4), scales=sc[:, lo:hi], in_=h[:, lo:hi, :].rearrange("p n t -> p (n t)")
+                out=codes[:, lo:hi].bitcast(FP8X4),
+                scales=scales[:, lo:hi],
+                in_=values[:, lo:hi, :].rearrange("p n t -> p (n t)"),
             )
 
         wa_bf = [held("wa_bf0", [P, R, SLOTS], BF16)]
 
-        def cast_wa(a, t, copy):
+        def cast_wa(a, t):
             src = wa_raw[a][:].rearrange("p j (g t u i) -> p t g u j i", t=4, u=2, i=4)
             dst = wa_bf[a][:].rearrange("p (t g u i) j -> p t g u j i", t=4, u=2, i=4)
-            copy(dst[:, t], src[:, t])
-
+            nc.scalar.copy(dst[:, t], src[:, t])
 
         for t in range(SLOTS):
-            cast_wa(0, t, nc.scalar.copy)
+            cast_wa(0, t)
 
         hb = held("hb", [P, J, SLOTS], BF16)
         hb_codes = held("hb_codes", [P, J], U32)
@@ -169,19 +161,19 @@ def tile_list_biaff_silu_bias_kernel(
                 for a in range(PASSES):
                     nc.tensor.matmul_mx(
                         zt,
-                        lhsT=wb_codes[:, a, 64 * t : 64 * (t + 1)].bitcast(FP4X4),
-                        lhsT_scale=wb_sc[:, a, 32 * t : 32 * (t + 1)].bitcast(U8),
+                        lhsT=wb_codes[:, a, P // 2 * t : P // 2 * (t + 1)].bitcast(FP4X4),
+                        lhsT_scale=wb_sc[:, a, P // 4 * t : P // 4 * (t + 1)].bitcast(U8),
                         rhs=vb_codes[:, a, 2 * HALF * h : 2 * HALF * (h + 1)].bitcast(FP4X4),
-                        rhs_scale=vb_sc[a][:, cols],
+                        rhs_scale=vb_sc[:, a, cols],
                         start=(a == 0),
                         stop=(a == PASSES - 1),
                     )
                 if t % 2 == 1:
                     nc.scalar.activation(act_b[:, t // 2, cols, :], z[:].rearrange("p (e n) -> p n e", e=2), SILU)
-            if h == 0:
-                s_bank = bank()
-                nc.tensor.transpose(s_bank[:, 0:P], s_rows[:], ident[:])
-                nc.vector.tensor_copy(s_cols[:], s_bank[:, 0 : 2 * SLOTS])
+
+        s_bank = bank()
+        nc.tensor.transpose(s_bank[:, 0:P], s_rows[:], ident[:])
+        nc.vector.tensor_copy(s_cols[:], s_bank[:, 0 : 2 * SLOTS])
 
         va_sc = held("va_sc", [P, M], U8, "wb_sc_raw")
         nc.vector.tensor_copy(va_sc[:], tab_sc[:].bitcast(U8).indirect(list_a[:]))
@@ -191,10 +183,10 @@ def tile_list_biaff_silu_bias_kernel(
         quantize(wa_bf[0], wa_codes[0], wa_sc[0], 0, R)
         va_codes = [held("va_codes0", [P, M], U32, "wa_bf0")]
 
-        def gather_a(a, h):
+        def gather_last_pass(h):
             nc.vector.tensor_copy(
-                va_codes[a][:, h * HALF : (h + 1) * HALF],
-                tab_w[a][:].bitcast(U32).indirect(list_a[:, 16 * h : 16 * (h + 1)]),
+                va_codes[1][:, h * HALF : (h + 1) * HALF],
+                tab_w[1][:].bitcast(U32).indirect(list_a[:, HALF // 16 * h : HALF // 16 * (h + 1)]),
             )
 
         def sums_a(z, a, h, t):
@@ -223,15 +215,15 @@ def tile_list_biaff_silu_bias_kernel(
                 sb_cols.rearrange("p (u e) -> p u e", e=2).unsqueeze(1).to_broadcast([P, HALF, 2, 2]),
                 MULT,
             )
-        quantize(hb, hb_codes, hb_sc, 0, J)
-        va_codes.append(held("va_codes1", [P, M], U32, "hb"))
+        va_codes.append(held("va_codes1", [P, M], U32, "act_b"))
         wa_bf.append(held("wa_bf1", [P, R, SLOTS], BF16, "vb_codes"))
         for t in range(SLOTS):
-            cast_wa(1, t, nc.scalar.copy)
-        gather_a(1, 0)
+            cast_wa(1, t)
+        gather_last_pass(0)
         quantize(wa_bf[1], wa_codes[1], wa_sc[1], 0, HALF)
-        gather_a(1, 1)
         quantize(wa_bf[1], wa_codes[1], wa_sc[1], HALF, R)
+        gather_last_pass(1)
+        quantize(hb, hb_codes, hb_sc, 0, J)
         act_a = held("act_a", [P, SLOTS, M], F32)
         for h in range(2):
             for t in range(SLOTS):
@@ -241,6 +233,15 @@ def tile_list_biaff_silu_bias_kernel(
         ha = held("ha", [P, M, SLOTS], BF16)
         ha_codes = held("ha_codes", [P, M], U32)
         ha_sc = held("ha_sc", [P, M], U8)
+
+        def scale_round_a(c):
+            cols = slice(c * CHUNK, (c + 1) * CHUNK)
+            nc.vector.tensor_tensor(
+                ha[:, cols, :].rearrange("p (n i) t -> p n t i", i=4),
+                act_a[:, :, cols].rearrange("p t (n i) -> p n t i", i=4),
+                sa_cols.unsqueeze(1).unsqueeze(3).to_broadcast([P, CHUNK // 4, SLOTS, 4]),
+                MULT,
+            )
 
         def score(c):
             cols = slice(c * CHUNK, (c + 1) * CHUNK)
@@ -262,11 +263,11 @@ def tile_list_biaff_silu_bias_kernel(
             nc.sync.dma_start(out[c * CHUNK : (c + 1) * CHUNK, :], res[:])
 
         ys = {}
-        for step in range(CHUNKS + 3):
+        for step in range(CHUNKS + FINISH_LAG):
             if step < CHUNKS:
-                scale_round(act_a, ha, step * CHUNK, (step + 1) * CHUNK, sa_cols)
+                scale_round_a(step)
             if 0 <= step - 1 < CHUNKS:
                 quantize(ha, ha_codes, ha_sc, (step - 1) * CHUNK, step * CHUNK)
                 ys[step - 1] = score(step - 1)
-            if 0 <= step - 3 < CHUNKS:
-                finish(step - 3, ys[step - 3])
+            if step >= FINISH_LAG:
+                finish(step - FINISH_LAG, ys[step - FINISH_LAG])

@@ -35,200 +35,231 @@ def tile_list_biaff_silu_bias_kernel(
     with ExitStack() as ctx:
         keep = ctx.enter_context(tc.tile_pool(name="keep", bufs=1))
         ring = ctx.enter_context(tc.tile_pool(name="ring", bufs=CHUNKS))
-        psum = ctx.enter_context(tc.psum_pool(name="psum", bufs=8))
+        psum = ctx.enter_context(tc.psum_pool(name="psum", bufs=1))
 
-        def bank():
-            return psum.tile([P, 512], F32, name="bank")
+        def bank(n):
+            return psum.tile([P, 512], F32, name="bank%d" % n, tag="bank%d" % n)
 
         def held(name, shape, dtype, slot=None):
             return keep.tile(shape, dtype, name=name, tag=slot or name, align_bytes=64)
 
         list_a = keep.tile([P, M // 16], U16, name="list_a")
         list_b = keep.tile([P, J // 16], U16, name="list_b")
-        tab2_sc = [held("tab2_sc%d" % a, [P, T // 4], I32) for a in range(PASSES)]
+        tab2_sc = held("tab2_sc", [P, T // 4], I32)
+        vb_sc1 = held("vb_sc1", [P, J // 4], I32)
         tab_sc = held("tab_sc", [P, T // 4], I32)
         wb_sc_raw = held("wb_sc_raw", [P, PASSES, R // 4], I32)
+        sb_rows = held("sb_rows", [P, P], F32)
         s_rows = held("s_rows", [P, P], F32)
+        warm_in = held("warm_in", [P, 8], F32)
         warm = held("warm", [P, 1], F32)
         ident = held("ident", [P, P], F32)
         tab2_w = held("tab2_w", [P, T], I32)
         wb_raw = held("wb_raw", [P, PASSES, R // 2], I32)
-        wa_raw = [held("wa_raw%d" % a, [P, SLOTS, R], F32) for a in range(PASSES)]
-        tab_w = [held("tab_w%d" % a, [P, T], I32) for a in range(PASSES)]
-        b_col = held("b_col", [P, 4], F32)
+        wa_raw = [held("wa_raw0", [P, SLOTS, R], F32)]
+        tab_w = []
 
-        nc.gpsimd.memset(tab2_sc[0][:], 0)
-        nc.vector.memset(tab2_sc[1][:], 0)
+        nc.gpsimd.memset(tab2_sc[:], 0)
         nc.vector.memset(wb_sc_raw[:], 0)
-        nc.vector.memset(s_rows[:], 0.0)
+        nc.gpsimd.memset(sb_rows[:], 0.0)
+        nc.vector.memset(warm_in[:], 0.0)
         nc.vector.memset(tab_sc[:], 0)
-        make_identity(nc, ident[:])
-        nc.scalar.activation(warm[:], ident[:, 0:1], SILU)
+        nc.vector.memset(s_rows[:], 0.0)
+        nc.vector.memset(vb_sc1[:], 0)
+        nc.scalar.activation(warm[:], warm_in[:, 0:1], SILU)
 
-        def load_factor(row, vec):
-            nc.sync.dma_start(
-                s_rows[row : row + 4, :].rearrange("t (g i) -> t g i", i=8), vec.rearrange("(g t i) -> t g i", t=4, i=8)
+        def load_factor(rows, vec):
+            nc.gpsimd.dma_start(
+                rows[0:SLOTS, :].rearrange("t (g i) -> t g i", i=8), vec.rearrange("(g t i) -> t g i", t=4, i=8)
             )
 
-        def load_wa(a):
-            nc.sync.dma_start(wa_raw[a][:], wa[512 * a : 512 * (a + 1), :].rearrange("(p j) r -> p j r", j=4))
+        def wa_rows(a):
+            return wa[512 * a : 512 * (a + 1), :].rearrange("(p j) r -> p j r", j=4)
 
-        def load_tab(a):
+        def load_tab(a, slot):
+            tab_w.append(held("tab_w%d" % a, [P, T], I32, slot))
             nc.sync.dma_start(tab_w[a][:], tab_words[a].rearrange("p t i -> p (t i)").bitcast(I32))
+
+        make_identity(nc, ident[:])
+        load_factor(sb_rows, sb)
+        load_factor(s_rows, sa)
+        nc.gpsimd.dma_start(s_rows[SLOTS : 2 * SLOTS, :], b.rearrange("(c n) -> c n", n=P))
+        ts = tab_scales.bitcast(I32)
+
+        def load_tab_sc(q):
+            nc.sync.dma_start(tab_sc[32 * q + TAB_ROW[0] : 32 * q + TAB_ROW[1] + 4, :], ts[:, 4 * q : 4 * q + 4, :])
 
         nc.sync.dma_start(list_b[:], offs2)
         nc.sync.dma_start(list_a[:], offs)
-        nc.sync.dma_start(b_col[:], b.rearrange("(p c) -> p c", c=4))
-        t2s = tab2_scales.bitcast(I32).rearrange("a (q r) n -> a r q n", r=4)
-        for r in range(4):
-            nc.sync.dma_start(tab2_sc[0][r:P:32, :], t2s[0, r])
-        nc.sync.dma_start(tab2_w[:], tab2_words[0].rearrange("p t i -> p (t i)").bitcast(I32))
-        for r in range(4):
-            nc.sync.dma_start(tab2_sc[1][r:P:32, :], t2s[1, r])
         nc.sync.dma_start(wb_raw[:], wb_words.bitcast(I32).rearrange("a p n -> p a n"))
+        t2s = tab2_scales.bitcast(I32).rearrange("a (q r) n -> r q a n", r=4)
+        for r in range(4):
+            nc.sync.dma_start(tab2_sc[r:P:16, :], t2s[r])
+        nc.sync.dma_start(tab2_w[:], tab2_words[0].rearrange("p t i -> p (t i)").bitcast(I32))
         wbs = wb_scales.bitcast(I32).rearrange("a (q r) n -> r q a n", r=4)
-        nc.sync.dma_start(wb_sc_raw[0:P:32, :, :], wbs[0])
-        load_wa(0)
-        for r in range(1, 4):
+        for r in range(4):
             nc.sync.dma_start(wb_sc_raw[r:P:32, :, :], wbs[r])
-        ts = tab_scales.bitcast(I32)
-        for q in range(4):
-            nc.sync.dma_start(tab_sc[32 * q + TAB_ROW[0] : 32 * q + TAB_ROW[1] + 4, :], ts[:, 4 * q : 4 * q + 4, :])
-        load_tab(0)
-        load_factor(SLOTS, sb)
-        load_factor(0, sa)
-        load_wa(1)
-        load_tab(1)
+        nc.sync.dma_start(wa_raw[0][:], wa_rows(0))
 
-        vb_sc = held("vb_sc_all", [P, PASSES, J], U8)
-        nc.vector.tensor_copy(vb_sc[:, 0, :], tab2_sc[0][:].bitcast(U8).indirect(list_b[:]))
-        vb_pairs = held("vb_pairs", [P, J], U32)
-        nc.vector.tensor_copy(vb_pairs[:], tab2_w[:].bitcast(U32).indirect(list_b[:]))
-        vb_codes = held("vb_codes", [P, PASSES, 2 * J], U8)
-        nc.vector.tensor_copy(vb_sc[:, 1, :], tab2_sc[1][:].bitcast(U8).indirect(list_b[:]))
-        nc.vector.tensor_copy(
-            vb_codes[:].rearrange("p a n -> p (a n)").bitcast(U16).rearrange("p (a j) -> p a j", a=2),
-            vb_pairs[:].bitcast(U16).rearrange("p (j a) -> p a j", a=2),
-        )
+        vb_sc0 = held("vb_sc0", [P, J], U8)
+        nc.vector.tensor_copy(vb_sc0[:], tab2_sc[:].bitcast(U8).indirect(list_b[:]))
+        for q in range(4):
+            load_tab_sc(q)
+        nc.sync.dma_start(vb_sc1[0 : P - 16, :], vb_sc0[16:P, :].bitcast(I32))
+        vb_sc = [vb_sc0[:], vb_sc1[:].bitcast(U8)]
+        load_tab(0, "tab2_sc")
+
         wb_codes = held("wb_codes", [P, PASSES, R // 2], I32)
         wb_sc = held("wb_sc", [P, PASSES, R // 4], I32)
+        vb_pairs = held("vb_pairs", [P, J], U32)
+        vb_codes = held("vb_codes", [P, PASSES, 2 * J], U8)
+
+        def gather_b(h):
+            nc.vector.tensor_copy(
+                vb_pairs[:, h * HALF : (h + 1) * HALF],
+                tab2_w[:].bitcast(U32).indirect(list_b[:, HALF // 16 * h : HALF // 16 * (h + 1)]),
+            )
+
+        def part_b(h):
+            cols = slice(h * HALF, (h + 1) * HALF)
+            nc.vector.tensor_copy(
+                vb_codes[:].rearrange("p a n -> p (a n)").bitcast(U16).rearrange("p (a j) -> p a j", a=2)[:, :, cols],
+                vb_pairs[:].bitcast(U16).rearrange("p (j a) -> p a j", a=2)[:, :, cols],
+            )
+
         nc.vector.tensor_copy(
             wb_codes[:].rearrange("p a (t g w) -> p a t g w", t=4, w=4),
             wb_raw[:].rearrange("p a (g t w) -> p a t g w", t=4, w=4),
         )
+        gather_b(0)
         nc.vector.tensor_copy(
             wb_sc[:].rearrange("p a (t g w) -> p a t g w", t=4, w=2),
             wb_sc_raw[:].rearrange("p a (g t w) -> p a t g w", t=4, w=2),
         )
+        part_b(0)
+        gather_b(1)
+        wa_raw.append(held("wa_raw1", [P, SLOTS, R], F32, "tab2_w"))
+        nc.sync.dma_start(wa_raw[1][:], wa_rows(1))
+        part_b(1)
 
-        b_bank = bank()
-        for c in range(4):
-            nc.tensor.transpose(b_bank[:, c * P : (c + 1) * P], b_col[:, c : c + 1].to_broadcast([P, P]), ident[:])
-        b_all = held("b_all", [P, J], F32)
-        nc.scalar.copy(b_all[:].rearrange("p (n c) -> p n c", c=4), b_bank[:].rearrange("p (c n) -> p n c", c=4))
-
-        s_cols = held("s_cols", [P, 2 * SLOTS], F32)
-        sa_cols = s_cols[:, 0:SLOTS]
-        sb_cols = s_cols[:, SLOTS : 2 * SLOTS]
-
-        def quantize(values, codes, scales, lo, hi):
+        def quantize(values, codes, scales):
             nc.vector.quantize_mx(
-                out=codes[:, lo:hi].bitcast(FP8X4),
-                scales=scales[:, lo:hi],
-                in_=values[:, lo:hi, :].rearrange("p n t -> p (n t)"),
+                out=codes.bitcast(FP8X4),
+                scales=scales,
+                in_=values.rearrange("p n t -> p (n t)"),
             )
 
         wa_bf = [held("wa_bf0", [P, R, SLOTS], BF16)]
 
-        def cast_wa(a, t):
+        def cast_wa(copy, a, t):
             src = wa_raw[a][:].rearrange("p j (g t u i) -> p t g u j i", t=4, u=2, i=4)
             dst = wa_bf[a][:].rearrange("p (t g u i) j -> p t g u j i", t=4, u=2, i=4)
-            nc.scalar.copy(dst[:, t], src[:, t])
+            copy(dst[:, t], src[:, t])
 
         for t in range(SLOTS):
-            cast_wa(0, t)
+            cast_wa(nc.scalar.copy if t < 2 else nc.vector.tensor_copy, 0, t)
 
-        hb = held("hb", [P, J, SLOTS], BF16)
+        load_tab(1, "wa_raw0")
+
+        sb_cols = held("sb_cols", [P, SLOTS], F32)
+        sb_bank = bank(6)
+        nc.tensor.transpose(sb_bank[:, 0:P], sb_rows[:], ident[:])
+        nc.scalar.copy(sb_cols[:], sb_bank[:, 0:SLOTS])
+
+        hb = [held("hb0", [P, HALF, SLOTS], BF16)]
         hb_codes = held("hb_codes", [P, J], U32)
         hb_sc = held("hb_sc", [P, J], U8)
         act_b = held("act_b", [P, 2, J, 2], F32)
+        zb = [bank(n) for n in range(4)]
         for h in range(2):
             cols = slice(h * HALF, (h + 1) * HALF)
-            for t in range(SLOTS):
-                if t % 2 == 0:
-                    z = bank()
-                zt = z[:, (t % 2) * HALF : (t % 2 + 1) * HALF]
-                for a in range(PASSES):
+            for a in range(PASSES):
+                for t in range(SLOTS):
+                    z = zb[2 * h + t // 2]
                     nc.tensor.matmul_mx(
-                        zt,
+                        z[:, (t % 2) * HALF : (t % 2 + 1) * HALF],
                         lhsT=wb_codes[:, a, P // 2 * t : P // 2 * (t + 1)].bitcast(FP4X4),
                         lhsT_scale=wb_sc[:, a, P // 4 * t : P // 4 * (t + 1)].bitcast(U8),
                         rhs=vb_codes[:, a, 2 * HALF * h : 2 * HALF * (h + 1)].bitcast(FP4X4),
-                        rhs_scale=vb_sc[:, a, cols],
-                        start=(a == 0),
-                        stop=(a == PASSES - 1),
+                        rhs_scale=vb_sc[a][:, cols],
+                        start=(a == 0 and t % 2 == 0),
+                        stop=(a == PASSES - 1 and t % 2 == 1),
                     )
-                if t % 2 == 1:
-                    nc.scalar.activation(act_b[:, t // 2, cols, :], z[:].rearrange("p (e n) -> p n e", e=2), SILU)
-
-        s_bank = bank()
-        nc.tensor.transpose(s_bank[:, 0:P], s_rows[:], ident[:])
-        nc.vector.tensor_copy(s_cols[:], s_bank[:, 0 : 2 * SLOTS])
+                    if a == PASSES - 1 and t % 2 == 1:
+                        nc.scalar.activation(act_b[:, t // 2, cols, :], z[:].rearrange("p (e n) -> p n e", e=2), SILU)
 
         va_sc = held("va_sc", [P, M], U8, "wb_sc_raw")
         nc.vector.tensor_copy(va_sc[:], tab_sc[:].bitcast(U8).indirect(list_a[:]))
-        wa_codes = [held("wa_codes0", [P, R], U32, "tab_sc"), held("wa_codes1", [P, R], U32)]
+        wa_codes = [held("wa_codes0", [P, R], U32)]
         wa_sc = [held("wa_sc%d" % a, [P, R], U8) for a in range(PASSES)]
+        va_codes = [held("va_codes%d" % a, [P, M], U32) for a in range(PASSES)]
+        quantize(wa_bf[0][:], wa_codes[0][:], wa_sc[0][:])
 
-        quantize(wa_bf[0], wa_codes[0], wa_sc[0], 0, R)
-        va_codes = [held("va_codes0", [P, M], U32, "wa_bf0")]
-
-        def gather_last_pass(h):
-            nc.vector.tensor_copy(
-                va_codes[1][:, h * HALF : (h + 1) * HALF],
-                tab_w[1][:].bitcast(U32).indirect(list_a[:, HALF // 16 * h : HALF // 16 * (h + 1)]),
-            )
-
-        def sums_a(z, a, h, t):
-            cols = slice(h * HALF, (h + 1) * HALF)
-            nc.tensor.matmul_mx(
-                z[:, 0:HALF],
-                lhsT=wa_codes[a][:, P * t : P * (t + 1)].bitcast(FP8X4),
-                lhsT_scale=wa_sc[a][:, P * t : P * (t + 1)],
-                rhs=va_codes[a][:, cols].bitcast(FP8X4),
-                rhs_scale=va_sc[TAB_ROW[a] : P, cols],
-                start=(a == 0),
-                stop=(a == PASSES - 1),
-            )
-
-        za = {}
-        nc.vector.tensor_copy(va_codes[0][:], tab_w[0][:].bitcast(U32).indirect(list_a[:]))
-        for h in range(2):
-            for t in range(SLOTS):
-                za[h, t] = bank()
-                sums_a(za[h, t], 0, h, t)
-        for h in range(2):
+        def scale_round_b(h):
             cols = slice(h * HALF, (h + 1) * HALF)
             nc.vector.tensor_tensor(
-                hb[:, cols, :].rearrange("p n (u e) -> p n u e", e=2),
+                hb[h][:].rearrange("p n (u e) -> p n u e", e=2),
                 act_b[:, :, cols, :].rearrange("p u n e -> p n u e"),
-                sb_cols.rearrange("p (u e) -> p u e", e=2).unsqueeze(1).to_broadcast([P, HALF, 2, 2]),
+                sb_cols[:].rearrange("p (u e) -> p u e", e=2).unsqueeze(1).to_broadcast([P, HALF, 2, 2]),
                 MULT,
             )
-        va_codes.append(held("va_codes1", [P, M], U32, "act_b"))
+
+        def gather_words(a, h):
+            nc.vector.tensor_copy(
+                va_codes[a][:, h * HALF : (h + 1) * HALF],
+                tab_w[a][:].bitcast(U32).indirect(list_a[:, HALF // 16 * h : HALF // 16 * (h + 1)]),
+            )
+
+        def sums_a(z, a, c):
+            cols = slice(c * CHUNK, (c + 1) * CHUNK)
+            for t in range(SLOTS):
+                nc.tensor.matmul_mx(
+                    z[:, t * CHUNK : (t + 1) * CHUNK],
+                    lhsT=wa_codes[a][:, P * t : P * (t + 1)].bitcast(FP8X4),
+                    lhsT_scale=wa_sc[a][:, P * t : P * (t + 1)],
+                    rhs=va_codes[a][:, cols].bitcast(FP8X4),
+                    rhs_scale=va_sc[TAB_ROW[a] : P, cols],
+                    start=(a == 0 and t == 0),
+                    stop=(a == PASSES - 1 and t == SLOTS - 1),
+                )
+
+        scale_round_b(0)
         wa_bf.append(held("wa_bf1", [P, R, SLOTS], BF16, "vb_codes"))
         for t in range(SLOTS):
-            cast_wa(1, t)
-        gather_last_pass(0)
-        quantize(wa_bf[1], wa_codes[1], wa_sc[1], 0, HALF)
-        quantize(wa_bf[1], wa_codes[1], wa_sc[1], HALF, R)
-        gather_last_pass(1)
-        quantize(hb, hb_codes, hb_sc, 0, J)
-        act_a = held("act_a", [P, SLOTS, M], F32)
-        for h in range(2):
-            for t in range(SLOTS):
-                sums_a(za[h, t], 1, h, t)
-                nc.scalar.activation(act_a[:, t, h * HALF : (h + 1) * HALF], za[h, t][:, 0:HALF], SILU)
+            cast_wa(nc.scalar.copy, 1, t)
+        s_cols = held("s_cols", [P, 2 * SLOTS], F32, "tab2_w")
+        sa_cols = s_cols[:, 0:SLOTS]
+        s_bank = bank(3)
+        nc.tensor.transpose(s_bank[:, 0:P], s_rows[:], ident[:])
+        nc.scalar.copy(s_cols[:], s_bank[:, 0 : 2 * SLOTS])
+        b_bank = bank(2)
+        for c in range(4):
+            nc.tensor.transpose(
+                b_bank[:, c * P : (c + 1) * P], s_cols[:, SLOTS + c : SLOTS + c + 1].to_broadcast([P, P]), ident[:]
+            )
+        b_all = held("b_all", [P, J], F32)
+        nc.scalar.copy(b_all[:], b_bank[:])
+
+        gather_words(0, 0)
+        quantize(hb[0][:], hb_codes[:, 0:HALF], hb_sc[:, 0:HALF])
+        gather_words(0, 1)
+        hb.append(held("hb1", [P, HALF, SLOTS], BF16, "tab2_sc"))
+        scale_round_b(1)
+        za = [bank(4 + c) for c in range(CHUNKS)]
+        for c in range(CHUNKS):
+            sums_a(za[c], 0, c)
+        wa_codes.append(held("wa_codes1", [P, R], U32))
+        quantize(wa_bf[1][:, 0:HALF, :], wa_codes[1][:, 0:HALF], wa_sc[1][:, 0:HALF])
+        quantize(hb[1][:], hb_codes[:, HALF:J], hb_sc[:, HALF:J])
+        quantize(wa_bf[1][:, HALF:R, :], wa_codes[1][:, HALF:R], wa_sc[1][:, HALF:R])
+        gather_words(1, 0)
+        gather_words(1, 1)
+        act_a = held("act_a", [P, M, SLOTS], F32)
+        for c in range(CHUNKS):
+            sums_a(za[c], 1, c)
+            nc.scalar.activation(
+                act_a[:, c * CHUNK : (c + 1) * CHUNK, :], za[c][:].rearrange("p (t n) -> p n t", t=SLOTS), SILU
+            )
 
         ha = held("ha", [P, M, SLOTS], BF16)
         ha_codes = held("ha_codes", [P, M], U32)
@@ -237,15 +268,12 @@ def tile_list_biaff_silu_bias_kernel(
         def scale_round_a(c):
             cols = slice(c * CHUNK, (c + 1) * CHUNK)
             nc.vector.tensor_tensor(
-                ha[:, cols, :].rearrange("p (n i) t -> p n t i", i=4),
-                act_a[:, :, cols].rearrange("p t (n i) -> p n t i", i=4),
-                sa_cols.unsqueeze(1).unsqueeze(3).to_broadcast([P, CHUNK // 4, SLOTS, 4]),
-                MULT,
+                ha[:, cols, :], act_a[:, cols, :], sa_cols.unsqueeze(1).to_broadcast([P, CHUNK, SLOTS]), MULT
             )
 
         def score(c):
             cols = slice(c * CHUNK, (c + 1) * CHUNK)
-            y = bank()
+            y = bank(c)
             nc.tensor.matmul_mx(
                 y[:],
                 lhsT=ha_codes[:, cols].bitcast(FP8X4),
@@ -267,7 +295,8 @@ def tile_list_biaff_silu_bias_kernel(
             if step < CHUNKS:
                 scale_round_a(step)
             if 0 <= step - 1 < CHUNKS:
-                quantize(ha, ha_codes, ha_sc, (step - 1) * CHUNK, step * CHUNK)
+                cols = slice((step - 1) * CHUNK, step * CHUNK)
+                quantize(ha[:, cols, :], ha_codes[:, cols], ha_sc[:, cols])
                 ys[step - 1] = score(step - 1)
             if step >= FINISH_LAG:
                 finish(step - FINISH_LAG, ys[step - FINISH_LAG])

@@ -48,23 +48,22 @@ def tile_list_biaff_silu_bias_kernel(
         tab2_sc = held("tab2_sc", [P, T // 4], I32)
         vb_sc1 = held("vb_sc1", [P, J // 4], I32)
         tab_sc = held("tab_sc", [P, T // 4], I32)
-        wb_sc_raw = held("wb_sc_raw", [P, PASSES, R // 4], I32)
         sb_rows = held("sb_rows", [P, P], F32)
-        s_rows = held("s_rows", [P, P], F32)
+        sa_rows = held("sa_rows", [P, P], F32)
+        b_cols = held("b_cols", [P, SLOTS], F32)
         warm_in = held("warm_in", [P, 8], F32)
         warm = held("warm", [P, 1], F32)
         ident = held("ident", [P, P], F32)
         tab2_w = held("tab2_w", [P, T], I32)
         wb_raw = held("wb_raw", [P, PASSES, R // 2], I32)
-        wa_raw = [held("wa_raw0", [P, SLOTS, R], F32)]
-        tab_w = []
+        wa_raw = [held("wa_raw%d" % a, [P, SLOTS, R], F32) for a in range(PASSES)]
+        tab_w = [held("tab_w%d" % a, [P, T], I32) for a in range(PASSES)]
 
         nc.gpsimd.memset(tab2_sc[:], 0)
-        nc.vector.memset(wb_sc_raw[:], 0)
-        nc.gpsimd.memset(sb_rows[:], 0.0)
-        nc.vector.memset(warm_in[:], 0.0)
         nc.vector.memset(tab_sc[:], 0)
-        nc.vector.memset(s_rows[:], 0.0)
+        nc.vector.memset(warm_in[:], 0.0)
+        nc.vector.memset(sb_rows[:], 0.0)
+        nc.vector.memset(sa_rows[:], 0.0)
         nc.vector.memset(vb_sc1[:], 0)
         nc.scalar.activation(warm[:], warm_in[:, 0:1], SILU)
 
@@ -73,21 +72,13 @@ def tile_list_biaff_silu_bias_kernel(
                 rows[0:SLOTS, :].rearrange("t (g i) -> t g i", i=8), vec.rearrange("(g t i) -> t g i", t=4, i=8)
             )
 
-        def wa_rows(a):
-            return wa[512 * a : 512 * (a + 1), :].rearrange("(p j) r -> p j r", j=4)
-
-        def load_tab(a, slot):
-            tab_w.append(held("tab_w%d" % a, [P, T], I32, slot))
-            nc.sync.dma_start(tab_w[a][:], tab_words[a].rearrange("p t i -> p (t i)").bitcast(I32))
-
+        ts = tab_scales.bitcast(I32)
+        for q in range(4):
+            nc.gpsimd.dma_start(tab_sc[32 * q + TAB_ROW[0] : 32 * q + TAB_ROW[1] + 4, :], ts[:, 4 * q : 4 * q + 4, :])
         make_identity(nc, ident[:])
         load_factor(sb_rows, sb)
-        load_factor(s_rows, sa)
-        nc.gpsimd.dma_start(s_rows[SLOTS : 2 * SLOTS, :], b.rearrange("(c n) -> c n", n=P))
-        ts = tab_scales.bitcast(I32)
-
-        def load_tab_sc(q):
-            nc.sync.dma_start(tab_sc[32 * q + TAB_ROW[0] : 32 * q + TAB_ROW[1] + 4, :], ts[:, 4 * q : 4 * q + 4, :])
+        load_factor(sa_rows, sa)
+        nc.gpsimd.dma_start(b_cols[:], b.rearrange("(p c) -> p c", c=SLOTS))
 
         nc.sync.dma_start(list_b[:], offs2)
         nc.sync.dma_start(list_a[:], offs)
@@ -96,23 +87,25 @@ def tile_list_biaff_silu_bias_kernel(
         for r in range(4):
             nc.sync.dma_start(tab2_sc[r:P:16, :], t2s[r])
         nc.sync.dma_start(tab2_w[:], tab2_words[0].rearrange("p t i -> p (t i)").bitcast(I32))
-        wbs = wb_scales.bitcast(I32).rearrange("a (q r) n -> r q a n", r=4)
-        for r in range(4):
-            nc.sync.dma_start(wb_sc_raw[r:P:32, :, :], wbs[r])
-        nc.sync.dma_start(wa_raw[0][:], wa_rows(0))
+        for a in range(PASSES):
+            nc.sync.dma_start(wa_raw[a][:], wa[512 * a : 512 * (a + 1), :].rearrange("(p j) r -> p j r", j=4))
+        for a in range(PASSES):
+            nc.sync.dma_start(tab_w[a][:], tab_words[a].rearrange("p t i -> p (t i)").bitcast(I32))
 
         vb_sc0 = held("vb_sc0", [P, J], U8)
         nc.vector.tensor_copy(vb_sc0[:], tab2_sc[:].bitcast(U8).indirect(list_b[:]))
-        for q in range(4):
-            load_tab_sc(q)
-        nc.sync.dma_start(vb_sc1[0 : P - 16, :], vb_sc0[16:P, :].bitcast(I32))
+        nc.scalar.dma_start(vb_sc1[0 : P - 16, :], vb_sc0[16:P, :].bitcast(I32))
         vb_sc = [vb_sc0[:], vb_sc1[:].bitcast(U8)]
-        load_tab(0, "tab2_sc")
+        wb_sc_raw = held("wb_sc_raw", [P, PASSES, R // 4], I32, "tab2_sc")
+        nc.vector.memset(wb_sc_raw[:], 0)
+        wbs = wb_scales.bitcast(I32).rearrange("a (q r) n -> r q a n", r=4)
+        for r in range(4):
+            nc.scalar.dma_start(wb_sc_raw[r:P:32, :, :], wbs[r])
 
         wb_codes = held("wb_codes", [P, PASSES, R // 2], I32)
         wb_sc = held("wb_sc", [P, PASSES, R // 4], I32)
         vb_pairs = held("vb_pairs", [P, J], U32)
-        vb_codes = held("vb_codes", [P, PASSES, 2 * J], U8)
+        vb_codes = [held("vb_codes%d" % h, [P, PASSES, 2 * HALF], U8) for h in range(2)]
 
         def gather_b(h):
             nc.vector.tensor_copy(
@@ -123,7 +116,7 @@ def tile_list_biaff_silu_bias_kernel(
         def part_b(h):
             cols = slice(h * HALF, (h + 1) * HALF)
             nc.vector.tensor_copy(
-                vb_codes[:].rearrange("p a n -> p (a n)").bitcast(U16).rearrange("p (a j) -> p a j", a=2)[:, :, cols],
+                vb_codes[h][:].rearrange("p a n -> p (a n)").bitcast(U16).rearrange("p (a j) -> p a j", a=2),
                 vb_pairs[:].bitcast(U16).rearrange("p (j a) -> p a j", a=2)[:, :, cols],
             )
 
@@ -132,15 +125,15 @@ def tile_list_biaff_silu_bias_kernel(
             wb_raw[:].rearrange("p a (g t w) -> p a t g w", t=4, w=4),
         )
         gather_b(0)
+        part_b(0)
+        gather_b(1)
+        part_b(1)
         nc.vector.tensor_copy(
             wb_sc[:].rearrange("p a (t g w) -> p a t g w", t=4, w=2),
             wb_sc_raw[:].rearrange("p a (g t w) -> p a t g w", t=4, w=2),
         )
-        part_b(0)
-        gather_b(1)
-        wa_raw.append(held("wa_raw1", [P, SLOTS, R], F32, "tab2_w"))
-        nc.sync.dma_start(wa_raw[1][:], wa_rows(1))
-        part_b(1)
+        va_sc = held("va_sc", [P, M], U8, "vb_pairs")
+        nc.vector.tensor_copy(va_sc[:], tab_sc[:].bitcast(U8).indirect(list_a[:]))
 
         def quantize(values, codes, scales):
             nc.vector.quantize_mx(
@@ -149,7 +142,7 @@ def tile_list_biaff_silu_bias_kernel(
                 in_=values.rearrange("p n t -> p (n t)"),
             )
 
-        wa_bf = [held("wa_bf0", [P, R, SLOTS], BF16)]
+        wa_bf = [held("wa_bf%d" % a, [P, R, SLOTS], BF16) for a in range(PASSES)]
 
         def cast_wa(copy, a, t):
             src = wa_raw[a][:].rearrange("p j (g t u i) -> p t g u j i", t=4, u=2, i=4)
@@ -157,51 +150,40 @@ def tile_list_biaff_silu_bias_kernel(
             copy(dst[:, t], src[:, t])
 
         for t in range(SLOTS):
-            cast_wa(nc.scalar.copy if t < 2 else nc.vector.tensor_copy, 0, t)
+            cast_wa(nc.scalar.copy if t < 1 else nc.vector.tensor_copy, 0, t)
 
-        load_tab(1, "wa_raw0")
-
-        sb_cols = held("sb_cols", [P, SLOTS], F32)
-        sb_bank = bank(6)
+        sb_bank = bank(7)
         nc.tensor.transpose(sb_bank[:, 0:P], sb_rows[:], ident[:])
-        nc.scalar.copy(sb_cols[:], sb_bank[:, 0:SLOTS])
 
-        hb = [held("hb0", [P, HALF, SLOTS], BF16)]
+        hb = held("hb", [P, J, SLOTS], BF16)
         hb_codes = held("hb_codes", [P, J], U32)
         hb_sc = held("hb_sc", [P, J], U8)
-        act_b = held("act_b", [P, 2, J, 2], F32)
-        zb = [bank(n) for n in range(4)]
-        for h in range(2):
-            cols = slice(h * HALF, (h + 1) * HALF)
+        act_b = held("act_b", [P, J, SLOTS], F32)
+        for c in range(CHUNKS):
+            z = bank(c)
+            cols = slice(c * CHUNK, (c + 1) * CHUNK)
             for a in range(PASSES):
                 for t in range(SLOTS):
-                    z = zb[2 * h + t // 2]
                     nc.tensor.matmul_mx(
-                        z[:, (t % 2) * HALF : (t % 2 + 1) * HALF],
+                        z[:, t * CHUNK : (t + 1) * CHUNK],
                         lhsT=wb_codes[:, a, P // 2 * t : P // 2 * (t + 1)].bitcast(FP4X4),
                         lhsT_scale=wb_sc[:, a, P // 4 * t : P // 4 * (t + 1)].bitcast(U8),
-                        rhs=vb_codes[:, a, 2 * HALF * h : 2 * HALF * (h + 1)].bitcast(FP4X4),
+                        rhs=vb_codes[c // 2][:, a, 2 * CHUNK * (c % 2) : 2 * CHUNK * (c % 2 + 1)].bitcast(FP4X4),
                         rhs_scale=vb_sc[a][:, cols],
-                        start=(a == 0 and t % 2 == 0),
-                        stop=(a == PASSES - 1 and t % 2 == 1),
+                        start=(a == 0 and t == 0),
+                        stop=(a == PASSES - 1 and t == SLOTS - 1),
                     )
-                    if a == PASSES - 1 and t % 2 == 1:
-                        nc.scalar.activation(act_b[:, t // 2, cols, :], z[:].rearrange("p (e n) -> p n e", e=2), SILU)
+            nc.scalar.activation(act_b[:, cols, :], z[:].rearrange("p (t n) -> p n t", t=SLOTS), SILU)
 
-        va_sc = held("va_sc", [P, M], U8, "wb_sc_raw")
-        nc.vector.tensor_copy(va_sc[:], tab_sc[:].bitcast(U8).indirect(list_a[:]))
-        wa_codes = [held("wa_codes0", [P, R], U32)]
+        wa_codes = [held("wa_codes%d" % a, [P, R], U32) for a in range(PASSES)]
         wa_sc = [held("wa_sc%d" % a, [P, R], U8) for a in range(PASSES)]
         va_codes = [held("va_codes%d" % a, [P, M], U32) for a in range(PASSES)]
         quantize(wa_bf[0][:], wa_codes[0][:], wa_sc[0][:])
 
-        def scale_round_b(h):
-            cols = slice(h * HALF, (h + 1) * HALF)
+        def scale_round(dst, act, factors, c):
+            cols = slice(c * CHUNK, (c + 1) * CHUNK)
             nc.vector.tensor_tensor(
-                hb[h][:].rearrange("p n (u e) -> p n u e", e=2),
-                act_b[:, :, cols, :].rearrange("p u n e -> p n u e"),
-                sb_cols[:].rearrange("p (u e) -> p u e", e=2).unsqueeze(1).to_broadcast([P, HALF, 2, 2]),
-                MULT,
+                dst[:, cols, :], act[:, cols, :], factors[:, 0:SLOTS].unsqueeze(1).to_broadcast([P, CHUNK, SLOTS]), MULT
             )
 
         def gather_words(a, h):
@@ -223,35 +205,26 @@ def tile_list_biaff_silu_bias_kernel(
                     stop=(a == PASSES - 1 and t == SLOTS - 1),
                 )
 
-        scale_round_b(0)
-        wa_bf.append(held("wa_bf1", [P, R, SLOTS], BF16, "vb_codes"))
+        for c in range(CHUNKS):
+            scale_round(hb, act_b, sb_bank, c)
+        for h in range(2):
+            quantize(hb[:, h * HALF : (h + 1) * HALF, :], hb_codes[:, h * HALF : (h + 1) * HALF], hb_sc[:, h * HALF : (h + 1) * HALF])
         for t in range(SLOTS):
             cast_wa(nc.scalar.copy, 1, t)
-        s_cols = held("s_cols", [P, 2 * SLOTS], F32, "tab2_w")
-        sa_cols = s_cols[:, 0:SLOTS]
-        s_bank = bank(3)
-        nc.tensor.transpose(s_bank[:, 0:P], s_rows[:], ident[:])
-        nc.scalar.copy(s_cols[:], s_bank[:, 0 : 2 * SLOTS])
+        sa_bank = bank(3)
+        nc.tensor.transpose(sa_bank[:, 0:P], sa_rows[:], ident[:])
         b_bank = bank(2)
         for c in range(4):
-            nc.tensor.transpose(
-                b_bank[:, c * P : (c + 1) * P], s_cols[:, SLOTS + c : SLOTS + c + 1].to_broadcast([P, P]), ident[:]
-            )
+            nc.tensor.transpose(b_bank[:, c * P : (c + 1) * P], b_cols[:, c : c + 1].to_broadcast([P, P]), ident[:])
         b_all = held("b_all", [P, J], F32)
-        nc.scalar.copy(b_all[:], b_bank[:])
+        nc.scalar.copy(b_all[:].rearrange("p (n c) -> p n c", c=SLOTS), b_bank[:].rearrange("p (c n) -> p n c", c=SLOTS))
 
         gather_words(0, 0)
-        quantize(hb[0][:], hb_codes[:, 0:HALF], hb_sc[:, 0:HALF])
         gather_words(0, 1)
-        hb.append(held("hb1", [P, HALF, SLOTS], BF16, "tab2_sc"))
-        scale_round_b(1)
-        za = [bank(4 + c) for c in range(CHUNKS)]
+        za = [bank(n) for n in (4, 5, 6, 0)]
         for c in range(CHUNKS):
             sums_a(za[c], 0, c)
-        wa_codes.append(held("wa_codes1", [P, R], U32))
-        quantize(wa_bf[1][:, 0:HALF, :], wa_codes[1][:, 0:HALF], wa_sc[1][:, 0:HALF])
-        quantize(hb[1][:], hb_codes[:, HALF:J], hb_sc[:, HALF:J])
-        quantize(wa_bf[1][:, HALF:R, :], wa_codes[1][:, HALF:R], wa_sc[1][:, HALF:R])
+        quantize(wa_bf[1][:], wa_codes[1][:], wa_sc[1][:])
         gather_words(1, 0)
         gather_words(1, 1)
         act_a = held("act_a", [P, M, SLOTS], F32)
@@ -265,15 +238,9 @@ def tile_list_biaff_silu_bias_kernel(
         ha_codes = held("ha_codes", [P, M], U32)
         ha_sc = held("ha_sc", [P, M], U8)
 
-        def scale_round_a(c):
-            cols = slice(c * CHUNK, (c + 1) * CHUNK)
-            nc.vector.tensor_tensor(
-                ha[:, cols, :], act_a[:, cols, :], sa_cols.unsqueeze(1).to_broadcast([P, CHUNK, SLOTS]), MULT
-            )
-
         def score(c):
             cols = slice(c * CHUNK, (c + 1) * CHUNK)
-            y = bank(c)
+            y = bank((1, 4, 5, 6)[c])
             nc.tensor.matmul_mx(
                 y[:],
                 lhsT=ha_codes[:, cols].bitcast(FP8X4),
@@ -293,7 +260,7 @@ def tile_list_biaff_silu_bias_kernel(
         ys = {}
         for step in range(CHUNKS + FINISH_LAG):
             if step < CHUNKS:
-                scale_round_a(step)
+                scale_round(ha, act_a, sa_bank, step)
             if 0 <= step - 1 < CHUNKS:
                 cols = slice((step - 1) * CHUNK, step * CHUNK)
                 quantize(ha[:, cols, :], ha_codes[:, cols], ha_sc[:, cols])

@@ -34,6 +34,7 @@ def tile_list_biaff_silu_bias_kernel(
     nc = tc.nc
     with ExitStack() as ctx:
         keep = ctx.enter_context(tc.tile_pool(name="keep", bufs=1))
+        laid = ctx.enter_context(tc.tile_pool(name="laid", bufs=1))
         ring = ctx.enter_context(tc.tile_pool(name="ring", bufs=CHUNKS))
         psum = ctx.enter_context(tc.psum_pool(name="psum", bufs=1))
 
@@ -43,26 +44,30 @@ def tile_list_biaff_silu_bias_kernel(
         def held(name, shape, dtype, slot=None):
             return keep.tile(shape, dtype, name=name, tag=slot or name, align_bytes=64)
 
+        def placed(name, shape, dtype, offset):
+            return laid.tile(shape, dtype, name=name, offset=offset, align_bytes=64)
+
         list_a = keep.tile([P, M // 16], U16, name="list_a")
         list_b = keep.tile([P, J // 16], U16, name="list_b")
-        tab2_sc = held("tab2_sc", [P, T // 4], I32)
+        tab2_sc = placed("tab2_sc", [P, T // 4], I32, 8192)
         vb_sc1 = held("vb_sc1", [P, J // 4], I32)
-        tab_sc = held("tab_sc", [P, T // 4], I32)
+        va_sc1 = held("va_sc1", [P, M // 4], I32)
+        wb_sc_raw = held("wb_sc_raw", [P, PASSES, R // 4], I32)
         sb_rows = held("sb_rows", [P, P], F32)
         sa_rows = held("sa_rows", [P, P], F32)
-        b_cols = held("b_cols", [P, SLOTS], F32)
         warm_in = held("warm_in", [P, 8], F32)
         warm = held("warm", [P, 1], F32)
         ident = held("ident", [P, P], F32)
         tab2_w = held("tab2_w", [P, T], I32)
         wb_raw = held("wb_raw", [P, PASSES, R // 2], I32)
-        wa_raw = [held("wa_raw%d" % a, [P, SLOTS, R], F32) for a in range(PASSES)]
-        tab_w = [held("tab_w%d" % a, [P, T], I32) for a in range(PASSES)]
+        wa_raw = [held("wa_raw0", [P, SLOTS, R], F32)]
+        tab_w = []
 
         nc.gpsimd.memset(tab2_sc[:], 0)
-        nc.vector.memset(tab_sc[:], 0)
-        nc.vector.memset(warm_in[:], 0.0)
+        nc.gpsimd.memset(wb_sc_raw[:], 0)
         nc.vector.memset(sb_rows[:], 0.0)
+        nc.vector.memset(warm_in[:], 0.0)
+        nc.vector.memset(va_sc1[:], 0)
         nc.vector.memset(sa_rows[:], 0.0)
         nc.vector.memset(vb_sc1[:], 0)
         nc.scalar.activation(warm[:], warm_in[:, 0:1], SILU)
@@ -72,13 +77,9 @@ def tile_list_biaff_silu_bias_kernel(
                 rows[0:SLOTS, :].rearrange("t (g i) -> t g i", i=8), vec.rearrange("(g t i) -> t g i", t=4, i=8)
             )
 
-        ts = tab_scales.bitcast(I32)
-        for q in range(4):
-            nc.gpsimd.dma_start(tab_sc[32 * q + TAB_ROW[0] : 32 * q + TAB_ROW[1] + 4, :], ts[:, 4 * q : 4 * q + 4, :])
         make_identity(nc, ident[:])
         load_factor(sb_rows, sb)
         load_factor(sa_rows, sa)
-        nc.gpsimd.dma_start(b_cols[:], b.rearrange("(p c) -> p c", c=SLOTS))
 
         nc.sync.dma_start(list_b[:], offs2)
         nc.sync.dma_start(list_a[:], offs)
@@ -87,37 +88,44 @@ def tile_list_biaff_silu_bias_kernel(
         for r in range(4):
             nc.sync.dma_start(tab2_sc[r:P:16, :], t2s[r])
         nc.sync.dma_start(tab2_w[:], tab2_words[0].rearrange("p t i -> p (t i)").bitcast(I32))
-        for a in range(PASSES):
-            nc.sync.dma_start(wa_raw[a][:], wa[512 * a : 512 * (a + 1), :].rearrange("(p j) r -> p j r", j=4))
-        for a in range(PASSES):
-            nc.sync.dma_start(tab_w[a][:], tab_words[a].rearrange("p t i -> p (t i)").bitcast(I32))
-
-        vb_sc0 = held("vb_sc0", [P, J], U8)
-        nc.vector.tensor_copy(vb_sc0[:], tab2_sc[:].bitcast(U8).indirect(list_b[:]))
-        nc.scalar.dma_start(vb_sc1[0 : P - 16, :], vb_sc0[16:P, :].bitcast(I32))
-        vb_sc = [vb_sc0[:], vb_sc1[:].bitcast(U8)]
-        wb_sc_raw = held("wb_sc_raw", [P, PASSES, R // 4], I32, "tab2_sc")
-        nc.vector.memset(wb_sc_raw[:], 0)
         wbs = wb_scales.bitcast(I32).rearrange("a (q r) n -> r q a n", r=4)
         for r in range(4):
-            nc.scalar.dma_start(wb_sc_raw[r:P:32, :, :], wbs[r])
+            nc.sync.dma_start(wb_sc_raw[r:P:32, :, :], wbs[r])
+
+        def wa_rows(a):
+            return wa[512 * a : 512 * (a + 1), :].rearrange("(p j) r -> p j r", j=4)
+
+        def load_tab(a):
+            nc.sync.dma_start(tab_w[a][:], tab_words[a].rearrange("p t i -> p (t i)").bitcast(I32))
+
+        nc.sync.dma_start(wa_raw[0][:], wa_rows(0))
+        vb_sc0 = held("vb_sc0", [P, J], U8)
+        nc.vector.tensor_copy(vb_sc0[:], tab2_sc[:].bitcast(U8).indirect(list_b[:]))
+        nc.sync.dma_start(vb_sc1[0 : P - 16, :], vb_sc0[16:P, :].bitcast(I32))
+        vb_sc = [vb_sc0[:], vb_sc1[:].bitcast(U8)]
+        tab_sc = placed("tab_sc", [P, T // 4], I32, 7168)
+        nc.vector.memset(tab_sc[:], 0)
+        ts = tab_scales.bitcast(I32).rearrange("a (q r) n -> r q a n", r=4)
+        for r in range(4):
+            nc.sync.dma_start(tab_sc[r:P:16, :], ts[r])
+        tab_w.append(placed("tab_w0", [P, T], I32, 9216))
+        load_tab(0)
 
         wb_codes = held("wb_codes", [P, PASSES, R // 2], I32)
         wb_sc = held("wb_sc", [P, PASSES, R // 4], I32)
-        vb_pairs = held("vb_pairs", [P, J], U32)
+        vb_pairs = [held("vb_pairs0", [P, HALF], U32)]
         vb_codes = [held("vb_codes%d" % h, [P, PASSES, 2 * HALF], U8) for h in range(2)]
 
         def gather_b(h):
             nc.vector.tensor_copy(
-                vb_pairs[:, h * HALF : (h + 1) * HALF],
+                vb_pairs[h][:],
                 tab2_w[:].bitcast(U32).indirect(list_b[:, HALF // 16 * h : HALF // 16 * (h + 1)]),
             )
 
         def part_b(h):
-            cols = slice(h * HALF, (h + 1) * HALF)
             nc.vector.tensor_copy(
                 vb_codes[h][:].rearrange("p a n -> p (a n)").bitcast(U16).rearrange("p (a j) -> p a j", a=2),
-                vb_pairs[:].bitcast(U16).rearrange("p (j a) -> p a j", a=2)[:, :, cols],
+                vb_pairs[h][:].bitcast(U16).rearrange("p (j a) -> p a j", a=2),
             )
 
         nc.vector.tensor_copy(
@@ -126,14 +134,23 @@ def tile_list_biaff_silu_bias_kernel(
         )
         gather_b(0)
         part_b(0)
-        gather_b(1)
-        part_b(1)
         nc.vector.tensor_copy(
             wb_sc[:].rearrange("p a (t g w) -> p a t g w", t=4, w=2),
             wb_sc_raw[:].rearrange("p a (g t w) -> p a t g w", t=4, w=2),
         )
-        va_sc = held("va_sc", [P, M], U8, "vb_pairs")
-        nc.vector.tensor_copy(va_sc[:], tab_sc[:].bitcast(U8).indirect(list_a[:]))
+        vb_pairs.append(held("vb_pairs1", [P, HALF], U32, "wb_sc_raw"))
+        gather_b(1)
+        wa_raw.append(held("wa_raw1", [P, SLOTS, R], F32, "tab2_w"))
+        nc.sync.dma_start(wa_raw[1][:], wa_rows(1))
+        part_b(1)
+        tab_w.append(held("tab_w1", [P, T], I32, "wb_sc_raw"))
+        load_tab(1)
+        b_all = held("b_all", [P, J], F32, "vb_pairs0")
+        nc.sync.dma_start(b_all[:], b.partition_broadcast(P))
+        va_sc0 = held("va_sc0", [P, M], U8)
+        nc.vector.tensor_copy(va_sc0[:], tab_sc[:].bitcast(U8).indirect(list_a[:]))
+        nc.sync.dma_start(va_sc1[0 : P - 16, :], va_sc0[16:P, :].bitcast(I32))
+        va_sc = [va_sc0[:], va_sc1[:].bitcast(U8)]
 
         def quantize(values, codes, scales):
             nc.vector.quantize_mx(
@@ -150,39 +167,42 @@ def tile_list_biaff_silu_bias_kernel(
             copy(dst[:, t], src[:, t])
 
         for t in range(SLOTS):
-            cast_wa(nc.scalar.copy if t < 1 else nc.vector.tensor_copy, 0, t)
+            cast_wa(nc.scalar.copy if t < 2 else nc.vector.tensor_copy, 0, t)
 
         sb_bank = bank(7)
         nc.tensor.transpose(sb_bank[:, 0:P], sb_rows[:], ident[:])
+        sb_cols = held("sb_cols", [P, SLOTS], F32)
+        nc.scalar.copy(sb_cols[:], sb_bank[:, 0:SLOTS])
 
-        hb = held("hb", [P, J, SLOTS], BF16)
-        hb_codes = held("hb_codes", [P, J], U32)
+        hb = {1: held("hb1", [P, HALF, SLOTS], BF16)}
         hb_sc = held("hb_sc", [P, J], U8)
-        act_b = held("act_b", [P, J, SLOTS], F32)
-        for c in range(CHUNKS):
-            z = bank(c)
-            cols = slice(c * CHUNK, (c + 1) * CHUNK)
+        act_b = held("act_b", [P, 2, J, 2], F32)
+        for h in range(2):
+            cols = slice(h * HALF, (h + 1) * HALF)
+            zb = [bank(2 * h), bank(2 * h + 1)]
             for a in range(PASSES):
                 for t in range(SLOTS):
+                    z = zb[t // 2]
                     nc.tensor.matmul_mx(
-                        z[:, t * CHUNK : (t + 1) * CHUNK],
+                        z[:, (t % 2) * HALF : (t % 2 + 1) * HALF],
                         lhsT=wb_codes[:, a, P // 2 * t : P // 2 * (t + 1)].bitcast(FP4X4),
                         lhsT_scale=wb_sc[:, a, P // 4 * t : P // 4 * (t + 1)].bitcast(U8),
-                        rhs=vb_codes[c // 2][:, a, 2 * CHUNK * (c % 2) : 2 * CHUNK * (c % 2 + 1)].bitcast(FP4X4),
+                        rhs=vb_codes[h][:, a, :].bitcast(FP4X4),
                         rhs_scale=vb_sc[a][:, cols],
-                        start=(a == 0 and t == 0),
-                        stop=(a == PASSES - 1 and t == SLOTS - 1),
+                        start=(a == 0 and t % 2 == 0),
+                        stop=(a == PASSES - 1 and t % 2 == 1),
                     )
-            nc.scalar.activation(act_b[:, cols, :], z[:].rearrange("p (t n) -> p n t", t=SLOTS), SILU)
+                    if a == PASSES - 1 and t % 2 == 1:
+                        nc.scalar.activation(act_b[:, t // 2, cols, :], z[:].rearrange("p (e n) -> p n e", e=2), SILU)
 
         wa_codes = [held("wa_codes%d" % a, [P, R], U32) for a in range(PASSES)]
         wa_sc = [held("wa_sc%d" % a, [P, R], U8) for a in range(PASSES)]
         va_codes = [held("va_codes%d" % a, [P, M], U32) for a in range(PASSES)]
         quantize(wa_bf[0][:], wa_codes[0][:], wa_sc[0][:])
 
-        def scale_round(dst, act, factors, c):
+        def scale_round(engine, dst, act, factors, c):
             cols = slice(c * CHUNK, (c + 1) * CHUNK)
-            nc.vector.tensor_tensor(
+            engine.tensor_tensor(
                 dst[:, cols, :], act[:, cols, :], factors[:, 0:SLOTS].unsqueeze(1).to_broadcast([P, CHUNK, SLOTS]), MULT
             )
 
@@ -200,33 +220,40 @@ def tile_list_biaff_silu_bias_kernel(
                     lhsT=wa_codes[a][:, P * t : P * (t + 1)].bitcast(FP8X4),
                     lhsT_scale=wa_sc[a][:, P * t : P * (t + 1)],
                     rhs=va_codes[a][:, cols].bitcast(FP8X4),
-                    rhs_scale=va_sc[TAB_ROW[a] : P, cols],
+                    rhs_scale=va_sc[a][:, cols],
                     start=(a == 0 and t == 0),
                     stop=(a == PASSES - 1 and t == SLOTS - 1),
                 )
 
-        for c in range(CHUNKS):
-            scale_round(hb, act_b, sb_bank, c)
-        for h in range(2):
-            quantize(hb[:, h * HALF : (h + 1) * HALF, :], hb_codes[:, h * HALF : (h + 1) * HALF], hb_sc[:, h * HALF : (h + 1) * HALF])
-        for t in range(SLOTS):
-            cast_wa(nc.scalar.copy, 1, t)
-        sa_bank = bank(3)
-        nc.tensor.transpose(sa_bank[:, 0:P], sa_rows[:], ident[:])
-        b_bank = bank(2)
-        for c in range(4):
-            nc.tensor.transpose(b_bank[:, c * P : (c + 1) * P], b_cols[:, c : c + 1].to_broadcast([P, P]), ident[:])
-        b_all = held("b_all", [P, J], F32)
-        nc.scalar.copy(b_all[:].rearrange("p (n c) -> p n c", c=SLOTS), b_bank[:].rearrange("p (c n) -> p n c", c=SLOTS))
+        def scale_round_b(engine, factors, c):
+            engine.tensor_tensor(
+                hb[c // 2][:, (c % 2) * CHUNK : (c % 2 + 1) * CHUNK, :].rearrange("p n (u e) -> p n u e", e=2),
+                act_b[:, :, c * CHUNK : (c + 1) * CHUNK, :].rearrange("p u n e -> p n u e"),
+                factors[:, 0:SLOTS].rearrange("p (u e) -> p u e", e=2).unsqueeze(1).to_broadcast([P, CHUNK, 2, 2]),
+                MULT,
+            )
 
+        for c in range(2, 4):
+            scale_round_b(nc.gpsimd, sb_cols, c)
         gather_words(0, 0)
         gather_words(0, 1)
+        hb[0] = placed("hb0", [P, HALF, SLOTS], BF16, 9216)
+        for c in range(2):
+            scale_round_b(nc.vector, sb_bank, c)
         za = [bank(n) for n in (4, 5, 6, 0)]
         for c in range(CHUNKS):
             sums_a(za[c], 0, c)
+        for t in range(SLOTS):
+            cast_wa(nc.scalar.copy if t < 2 else nc.vector.tensor_copy, 1, t)
+        sa_bank = bank(1)
+        nc.tensor.transpose(sa_bank[:, 0:P], sa_rows[:], ident[:])
+
         quantize(wa_bf[1][:], wa_codes[1][:], wa_sc[1][:])
         gather_words(1, 0)
         gather_words(1, 1)
+        hb_codes = held("hb_codes", [P, J], U32, "wb_sc_raw")
+        for h in range(2):
+            quantize(hb[h][:], hb_codes[:, h * HALF : (h + 1) * HALF], hb_sc[:, h * HALF : (h + 1) * HALF])
         act_a = held("act_a", [P, M, SLOTS], F32)
         for c in range(CHUNKS):
             sums_a(za[c], 1, c)
@@ -240,7 +267,7 @@ def tile_list_biaff_silu_bias_kernel(
 
         def score(c):
             cols = slice(c * CHUNK, (c + 1) * CHUNK)
-            y = bank((1, 4, 5, 6)[c])
+            y = bank((2, 3, 4, 5)[c])
             nc.tensor.matmul_mx(
                 y[:],
                 lhsT=ha_codes[:, cols].bitcast(FP8X4),
@@ -260,7 +287,7 @@ def tile_list_biaff_silu_bias_kernel(
         ys = {}
         for step in range(CHUNKS + FINISH_LAG):
             if step < CHUNKS:
-                scale_round(ha, act_a, sa_bank, step)
+                scale_round(nc.vector, ha, act_a, sa_bank, step)
             if 0 <= step - 1 < CHUNKS:
                 cols = slice((step - 1) * CHUNK, step * CHUNK)
                 quantize(ha[:, cols, :], ha_codes[:, cols], ha_sc[:, cols])

@@ -145,12 +145,12 @@ def tile_list_biaff_silu_bias_kernel(
         part_b(1)
         tab_w.append(held("tab_w1", [P, T], I32, "wb_sc_raw"))
         load_tab(1)
-        b_all = held("b_all", [P, J], F32, "vb_pairs0")
-        nc.sync.dma_start(b_all[:], b.partition_broadcast(P))
         va_sc0 = held("va_sc0", [P, M], U8)
         nc.vector.tensor_copy(va_sc0[:], tab_sc[:].bitcast(U8).indirect(list_a[:]))
         nc.sync.dma_start(va_sc1[0 : P - 16, :], va_sc0[16:P, :].bitcast(I32))
         va_sc = [va_sc0[:], va_sc1[:].bitcast(U8)]
+        b_all = held("b_all", [P, J], F32, "vb_pairs0")
+        nc.sync.dma_start(b_all[:], b.partition_broadcast(P))
 
         def quantize(values, codes, scales):
             nc.vector.quantize_mx(

@@ -55,8 +55,6 @@ def tile_list_biaff_silu_bias_kernel(
         wb_sc_raw = held("wb_sc_raw", [P, PASSES, R // 4], I32)
         sb_rows = held("sb_rows", [P, P], F32)
         sa_rows = held("sa_rows", [P, P], F32)
-        warm_in = held("warm_in", [P, 8], F32)
-        warm = held("warm", [P, 1], F32)
         ident = held("ident", [P, P], F32)
         tab2_w = held("tab2_w", [P, T], I32)
         wb_raw = held("wb_raw", [P, PASSES, R // 2], I32)
@@ -66,11 +64,9 @@ def tile_list_biaff_silu_bias_kernel(
         nc.gpsimd.memset(tab2_sc[:], 0)
         nc.gpsimd.memset(wb_sc_raw[:], 0)
         nc.vector.memset(sb_rows[:], 0.0)
-        nc.vector.memset(warm_in[:], 0.0)
         nc.vector.memset(va_sc1[:], 0)
         nc.vector.memset(sa_rows[:], 0.0)
         nc.vector.memset(vb_sc1[:], 0)
-        nc.scalar.activation(warm[:], warm_in[:, 0:1], SILU)
 
         def load_factor(rows, vec):
             nc.gpsimd.dma_start(
@@ -108,8 +104,8 @@ def tile_list_biaff_silu_bias_kernel(
         ts = tab_scales.bitcast(I32).rearrange("a (q r) n -> r q a n", r=4)
         for r in range(4):
             nc.sync.dma_start(tab_sc[r:P:16, :], ts[r])
-        tab_w.append(placed("tab_w0", [P, T], I32, 9216))
-        load_tab(0)
+        wa_raw.append(placed("wa_raw1", [P, SLOTS, R], F32, 9216))
+        nc.sync.dma_start(wa_raw[1][:], wa_rows(1))
 
         wb_codes = held("wb_codes", [P, PASSES, R // 2], I32)
         wb_sc = held("wb_sc", [P, PASSES, R // 4], I32)
@@ -140,8 +136,8 @@ def tile_list_biaff_silu_bias_kernel(
         )
         vb_pairs.append(held("vb_pairs1", [P, HALF], U32, "wb_sc_raw"))
         gather_b(1)
-        wa_raw.append(held("wa_raw1", [P, SLOTS, R], F32, "tab2_w"))
-        nc.sync.dma_start(wa_raw[1][:], wa_rows(1))
+        tab_w.append(held("tab_w0", [P, T], I32, "tab2_w"))
+        load_tab(0)
         part_b(1)
         tab_w.append(held("tab_w1", [P, T], I32, "wb_sc_raw"))
         load_tab(1)
@@ -174,7 +170,7 @@ def tile_list_biaff_silu_bias_kernel(
         sb_cols = held("sb_cols", [P, SLOTS], F32)
         nc.scalar.copy(sb_cols[:], sb_bank[:, 0:SLOTS])
 
-        hb = {1: held("hb1", [P, HALF, SLOTS], BF16)}
+        hb = {}
         hb_sc = held("hb_sc", [P, J], U8)
         act_b = held("act_b", [P, 2, J, 2], F32)
         for h in range(2):
@@ -233,22 +229,23 @@ def tile_list_biaff_silu_bias_kernel(
                 MULT,
             )
 
+        for t in range(SLOTS):
+            cast_wa(nc.vector.tensor_copy, 1, t)
+        quantize(wa_bf[1][:], wa_codes[1][:], wa_sc[1][:])
+        hb[1] = held("hb1", [P, HALF, SLOTS], BF16, "wa_bf1")
         for c in range(2, 4):
             scale_round_b(nc.gpsimd, sb_cols, c)
         gather_words(0, 0)
         gather_words(0, 1)
-        hb[0] = placed("hb0", [P, HALF, SLOTS], BF16, 9216)
+        hb[0] = held("hb0", [P, HALF, SLOTS], BF16, "tab2_w")
         for c in range(2):
             scale_round_b(nc.vector, sb_bank, c)
         za = [bank(n) for n in (4, 5, 6, 0)]
         for c in range(CHUNKS):
             sums_a(za[c], 0, c)
-        for t in range(SLOTS):
-            cast_wa(nc.scalar.copy if t < 2 else nc.vector.tensor_copy, 1, t)
         sa_bank = bank(1)
         nc.tensor.transpose(sa_bank[:, 0:P], sa_rows[:], ident[:])
 
-        quantize(wa_bf[1][:], wa_codes[1][:], wa_sc[1][:])
         gather_words(1, 0)
         gather_words(1, 1)
         hb_codes = held("hb_codes", [P, J], U32, "wb_sc_raw")

@@ -17,6 +17,7 @@ FP4X4 = mybir.dt.float4_e2m1fn_x4
 MULT = mybir.AluOpType.mult
 ADD = mybir.AluOpType.add
 SILU = mybir.ActivationFunctionType.Silu
+COPY = mybir.ActivationFunctionType.Copy
 
 P = 128
 PASSES = K // 512
@@ -77,9 +78,9 @@ def tile_list_biaff_silu_bias_kernel(
         load_factor(sb_rows, sb)
         load_factor(sa_rows, sa)
 
+        nc.sync.dma_start(wb_raw[:], wb_words.bitcast(I32).rearrange("a p n -> p a n"))
         nc.sync.dma_start(list_b[:], offs2)
         nc.sync.dma_start(list_a[:], offs)
-        nc.sync.dma_start(wb_raw[:], wb_words.bitcast(I32).rearrange("a p n -> p a n"))
         t2s = tab2_scales.bitcast(I32).rearrange("a (q r) n -> r q a n", r=4)
         for r in range(4):
             nc.sync.dma_start(tab2_sc[r:P:16, :], t2s[r])
@@ -191,6 +192,10 @@ def tile_list_biaff_silu_bias_kernel(
                     if a == PASSES - 1 and t % 2 == 1:
                         nc.scalar.activation(act_b[:, t // 2, cols, :], z[:].rearrange("p (e n) -> p n e", e=2), SILU)
 
+        hb[0] = held("hb0", [P, HALF, SLOTS], BF16)
+        for t in range(SLOTS):
+            nc.scalar.activation(hb[0][:, :, t], act_b[:, t // 2, 0:HALF, t % 2], COPY, scale=sb_cols[:, t : t + 1])
+
         wa_codes = [held("wa_codes%d" % a, [P, R], U32) for a in range(PASSES)]
         wa_sc = [held("wa_sc%d" % a, [P, R], U8) for a in range(PASSES)]
         va_codes = [held("va_codes%d" % a, [P, M], U32) for a in range(PASSES)]
@@ -232,14 +237,11 @@ def tile_list_biaff_silu_bias_kernel(
         for t in range(SLOTS):
             cast_wa(nc.vector.tensor_copy, 1, t)
         quantize(wa_bf[1][:], wa_codes[1][:], wa_sc[1][:])
-        hb[1] = held("hb1", [P, HALF, SLOTS], BF16, "wa_bf1")
-        for c in range(2, 4):
-            scale_round_b(nc.gpsimd, sb_cols, c)
         gather_words(0, 0)
         gather_words(0, 1)
-        hb[0] = held("hb0", [P, HALF, SLOTS], BF16, "tab2_w")
-        for c in range(2):
-            scale_round_b(nc.vector, sb_bank, c)
+        hb[1] = held("hb1", [P, HALF, SLOTS], BF16, "tab2_w")
+        scale_round_b(nc.vector, sb_bank, 2)
+        scale_round_b(nc.gpsimd, sb_cols, 3)
         za = [bank(n) for n in (4, 5, 6, 0)]
         for c in range(CHUNKS):
             sums_a(za[c], 0, c)

@@ -163,8 +163,16 @@ def tile_list_biaff_silu_bias_kernel(
             dst = wa_bf[a][:].rearrange("p (t g u i) j -> p t g u j i", t=4, u=2, i=4)
             copy(dst[:, t], src[:, t])
 
+        def cast_wa_gpsimd(a, t):
+            src = wa_raw[a][:].rearrange("p j (g t i) -> p t g i j", t=4, i=8)
+            dst = wa_bf[a][:].rearrange("p (t g i) j -> p t g i j", t=4, i=8)
+            nc.gpsimd.tensor_scalar(dst[:, t], src[:, t], 1.0, 0.0, MULT, ADD)
+
         for t in range(SLOTS):
-            cast_wa(nc.scalar.copy if t < 2 else nc.vector.tensor_copy, 0, t)
+            if t < 2:
+                cast_wa(nc.scalar.copy, 0, t)
+            else:
+                cast_wa_gpsimd(0, t)
 
         sb_bank = bank(7)
         nc.tensor.transpose(sb_bank[:, 0:P], sb_rows[:], ident[:])
@@ -196,7 +204,7 @@ def tile_list_biaff_silu_bias_kernel(
         for t in range(SLOTS):
             nc.scalar.activation(hb[0][:, :, t], act_b[:, t // 2, 0:HALF, t % 2], COPY, scale=sb_cols[:, t : t + 1])
 
-        wa_codes = [held("wa_codes%d" % a, [P, R], U32) for a in range(PASSES)]
+        wa_codes = [placed("wa_codes0", [P, R], U32, 7168), held("wa_codes1", [P, R], U32)]
         wa_sc = [held("wa_sc%d" % a, [P, R], U8) for a in range(PASSES)]
         va_codes = [held("va_codes%d" % a, [P, M], U32) for a in range(PASSES)]
         quantize(wa_bf[0][:], wa_codes[0][:], wa_sc[0][:])
@@ -239,8 +247,8 @@ def tile_list_biaff_silu_bias_kernel(
         quantize(wa_bf[1][:], wa_codes[1][:], wa_sc[1][:])
         gather_words(0, 0)
         gather_words(0, 1)
-        hb[1] = held("hb1", [P, HALF, SLOTS], BF16, "tab2_w")
-        scale_round_b(nc.vector, sb_bank, 2)
+        hb[1] = held("hb1", [P, HALF, SLOTS], BF16, "wa_bf1")
+        scale_round_b(nc.gpsimd, sb_cols, 2)
         scale_round_b(nc.gpsimd, sb_cols, 3)
         za = [bank(n) for n in (4, 5, 6, 0)]
         for c in range(CHUNKS):

@@ -52,10 +52,9 @@ def tile_list_biaff_silu_bias_kernel(
         list_b = keep.tile([P, J // 16], U16, name="list_b")
         tab2_sc = placed("tab2_sc", [P, T // 4], I32, 8192)
         vb_sc1 = held("vb_sc1", [P, J // 4], I32)
-        va_sc1 = held("va_sc1", [P, M // 4], I32)
-        wb_sc_raw = held("wb_sc_raw", [P, PASSES, R // 4], I32)
-        sb_rows = held("sb_rows", [P, P], F32)
-        sa_rows = held("sa_rows", [P, P], F32)
+        tab_sc = placed("tab_sc", [P, T // 4], I32, 0)
+        wb_sc_raw = placed("wb_sc_raw", [P, PASSES, R // 4], I32, 18432)
+        factor_rows = held("factor_rows", [P, P], F32)
         ident = held("ident", [P, P], F32)
         tab2_w = held("tab2_w", [P, T], I32)
         wb_raw = held("wb_raw", [P, PASSES, R // 2], I32)
@@ -63,20 +62,21 @@ def tile_list_biaff_silu_bias_kernel(
         tab_w = []
 
         nc.gpsimd.memset(tab2_sc[:], 0)
-        nc.gpsimd.memset(wb_sc_raw[:], 0)
-        nc.vector.memset(sb_rows[:], 0.0)
-        nc.vector.memset(va_sc1[:], 0)
-        nc.vector.memset(sa_rows[:], 0.0)
+        nc.gpsimd.memset(tab_sc[:], 0)
+        nc.vector.memset(wb_sc_raw[:], 0)
+        nc.vector.memset(factor_rows[:], 0.0)
         nc.vector.memset(vb_sc1[:], 0)
 
-        def load_factor(rows, vec):
-            nc.gpsimd.dma_start(
-                rows[0:SLOTS, :].rearrange("t (g i) -> t g i", i=8), vec.rearrange("(g t i) -> t g i", t=4, i=8)
+        def load_factor(row, vec):
+            nc.sync.dma_start(
+                factor_rows[row : row + SLOTS, :].rearrange("t (g i) -> t g i", i=8),
+                vec.rearrange("(g t i) -> t g i", t=4, i=8),
             )
 
+        ts = tab_scales.bitcast(I32).rearrange("a (q r) n -> q a r n", r=4)
+        for q in range(4):
+            nc.gpsimd.dma_start(tab_sc[32 * q + TAB_ROW[0] : 32 * q + TAB_ROW[0] + 8, :], ts[q])
         make_identity(nc, ident[:])
-        load_factor(sb_rows, sb)
-        load_factor(sa_rows, sa)
 
         nc.sync.dma_start(wb_raw[:], wb_words.bitcast(I32).rearrange("a p n -> p a n"))
         nc.sync.dma_start(list_b[:], offs2)
@@ -100,11 +100,8 @@ def tile_list_biaff_silu_bias_kernel(
         nc.vector.tensor_copy(vb_sc0[:], tab2_sc[:].bitcast(U8).indirect(list_b[:]))
         nc.sync.dma_start(vb_sc1[0 : P - 16, :], vb_sc0[16:P, :].bitcast(I32))
         vb_sc = [vb_sc0[:], vb_sc1[:].bitcast(U8)]
-        tab_sc = placed("tab_sc", [P, T // 4], I32, 7168)
-        nc.vector.memset(tab_sc[:], 0)
-        ts = tab_scales.bitcast(I32).rearrange("a (q r) n -> r q a n", r=4)
-        for r in range(4):
-            nc.sync.dma_start(tab_sc[r:P:16, :], ts[r])
+        load_factor(0, sb)
+        load_factor(SLOTS, sa)
         wa_raw.append(placed("wa_raw1", [P, SLOTS, R], F32, 9216))
         nc.sync.dma_start(wa_raw[1][:], wa_rows(1))
 
@@ -135,17 +132,15 @@ def tile_list_biaff_silu_bias_kernel(
             wb_sc[:].rearrange("p a (t g w) -> p a t g w", t=4, w=2),
             wb_sc_raw[:].rearrange("p a (g t w) -> p a t g w", t=4, w=2),
         )
-        vb_pairs.append(held("vb_pairs1", [P, HALF], U32, "wb_sc_raw"))
+        vb_pairs.append(placed("vb_pairs1", [P, HALF], U32, 18432))
         gather_b(1)
         tab_w.append(held("tab_w0", [P, T], I32, "tab2_w"))
         load_tab(0)
         part_b(1)
-        tab_w.append(held("tab_w1", [P, T], I32, "wb_sc_raw"))
+        tab_w.append(placed("tab_w1", [P, T], I32, 18944))
         load_tab(1)
-        va_sc0 = held("va_sc0", [P, M], U8)
+        va_sc0 = placed("va_sc0", [P, M], U8, 18432)
         nc.vector.tensor_copy(va_sc0[:], tab_sc[:].bitcast(U8).indirect(list_a[:]))
-        nc.sync.dma_start(va_sc1[0 : P - 16, :], va_sc0[16:P, :].bitcast(I32))
-        va_sc = [va_sc0[:], va_sc1[:].bitcast(U8)]
         b_all = held("b_all", [P, J], F32, "vb_pairs0")
         nc.sync.dma_start(b_all[:], b.partition_broadcast(P))
 
@@ -174,10 +169,6 @@ def tile_list_biaff_silu_bias_kernel(
             else:
                 cast_wa_gpsimd(0, t)
 
-        sb_bank = bank(7)
-        nc.tensor.transpose(sb_bank[:, 0:P], sb_rows[:], ident[:])
-        sb_cols = held("sb_cols", [P, SLOTS], F32)
-        nc.scalar.copy(sb_cols[:], sb_bank[:, 0:SLOTS])
 
         hb = {}
         hb_sc = held("hb_sc", [P, J], U8)
@@ -200,11 +191,18 @@ def tile_list_biaff_silu_bias_kernel(
                     if a == PASSES - 1 and t % 2 == 1:
                         nc.scalar.activation(act_b[:, t // 2, cols, :], z[:].rearrange("p (e n) -> p n e", e=2), SILU)
 
+        factor_bank = bank(1)
+        nc.tensor.transpose(factor_bank[:, 0:P], factor_rows[:], ident[:])
+        sb_bank = factor_bank[:, 0:SLOTS]
+        sa_bank = factor_bank[:, SLOTS : 2 * SLOTS]
+        sb_cols = held("sb_cols", [P, SLOTS], F32)
+        nc.scalar.copy(sb_cols[:], sb_bank)
+
         hb[0] = held("hb0", [P, HALF, SLOTS], BF16)
         for t in range(SLOTS):
             nc.scalar.activation(hb[0][:, :, t], act_b[:, t // 2, 0:HALF, t % 2], COPY, scale=sb_cols[:, t : t + 1])
 
-        wa_codes = [placed("wa_codes0", [P, R], U32, 7168), held("wa_codes1", [P, R], U32)]
+        wa_codes = [placed("wa_codes0", [P, R], U32, 0), held("wa_codes1", [P, R], U32)]
         wa_sc = [held("wa_sc%d" % a, [P, R], U8) for a in range(PASSES)]
         va_codes = [held("va_codes%d" % a, [P, M], U32) for a in range(PASSES)]
         quantize(wa_bf[0][:], wa_codes[0][:], wa_sc[0][:])
@@ -229,7 +227,7 @@ def tile_list_biaff_silu_bias_kernel(
                     lhsT=wa_codes[a][:, P * t : P * (t + 1)].bitcast(FP8X4),
                     lhsT_scale=wa_sc[a][:, P * t : P * (t + 1)],
                     rhs=va_codes[a][:, cols].bitcast(FP8X4),
-                    rhs_scale=va_sc[a][:, cols],
+                    rhs_scale=va_sc0[TAB_ROW[a] : P, cols],
                     start=(a == 0 and t == 0),
                     stop=(a == PASSES - 1 and t == SLOTS - 1),
                 )
@@ -250,15 +248,13 @@ def tile_list_biaff_silu_bias_kernel(
         hb[1] = held("hb1", [P, HALF, SLOTS], BF16, "wa_bf1")
         scale_round_b(nc.gpsimd, sb_cols, 2)
         scale_round_b(nc.gpsimd, sb_cols, 3)
-        za = [bank(n) for n in (4, 5, 6, 0)]
+        za = [bank(n) for n in (4, 5, 6, 7)]
         for c in range(CHUNKS):
             sums_a(za[c], 0, c)
-        sa_bank = bank(1)
-        nc.tensor.transpose(sa_bank[:, 0:P], sa_rows[:], ident[:])
 
         gather_words(1, 0)
         gather_words(1, 1)
-        hb_codes = held("hb_codes", [P, J], U32, "wb_sc_raw")
+        hb_codes = placed("hb_codes", [P, J], U32, 18944)
         for h in range(2):
             quantize(hb[h][:], hb_codes[:, h * HALF : (h + 1) * HALF], hb_sc[:, h * HALF : (h + 1) * HALF])
         act_a = held("act_a", [P, M, SLOTS], F32)
@@ -274,7 +270,7 @@ def tile_list_biaff_silu_bias_kernel(
 
         def score(c):
             cols = slice(c * CHUNK, (c + 1) * CHUNK)
-            y = bank((2, 3, 4, 5)[c])
+            y = bank((0, 2, 3, 4)[c])
             nc.tensor.matmul_mx(
                 y[:],
                 lhsT=ha_codes[:, cols].bitcast(FP8X4),

@@ -26,6 +26,7 @@ CHUNK = 128
 CHUNKS = M // CHUNK
 HALF = 256
 TAB_ROW = (8, 12)
+GPSIMD_COLS = 32
 FINISH_LAG = 3
 
 
@@ -193,10 +194,11 @@ def tile_list_biaff_silu_bias_kernel(
 
         factor_bank = bank(1)
         nc.tensor.transpose(factor_bank[:, 0:P], factor_rows[:], ident[:])
-        sb_bank = factor_bank[:, 0:SLOTS]
         sa_bank = factor_bank[:, SLOTS : 2 * SLOTS]
-        sb_cols = held("sb_cols", [P, SLOTS], F32)
-        nc.scalar.copy(sb_cols[:], sb_bank)
+        factor_cols = held("factor_cols", [P, 2 * SLOTS], F32)
+        nc.scalar.copy(factor_cols[:], factor_bank[:, 0 : 2 * SLOTS])
+        sb_cols = factor_cols[:, 0:SLOTS]
+        sa_cols = factor_cols[:, SLOTS : 2 * SLOTS]
 
         hb[0] = held("hb0", [P, HALF, SLOTS], BF16)
         for t in range(SLOTS):
@@ -207,10 +209,9 @@ def tile_list_biaff_silu_bias_kernel(
         va_codes = [held("va_codes%d" % a, [P, M], U32) for a in range(PASSES)]
         quantize(wa_bf[0][:], wa_codes[0][:], wa_sc[0][:])
 
-        def scale_round(engine, dst, act, factors, c):
-            cols = slice(c * CHUNK, (c + 1) * CHUNK)
+        def scale_round(engine, dst, act, factors, lo, hi):
             engine.tensor_tensor(
-                dst[:, cols, :], act[:, cols, :], factors[:, 0:SLOTS].unsqueeze(1).to_broadcast([P, CHUNK, SLOTS]), MULT
+                dst[:, lo:hi, :], act[:, lo:hi, :], factors[:, 0:SLOTS].unsqueeze(1).to_broadcast([P, hi - lo, SLOTS]), MULT
             )
 
         def gather_words(a, h):
@@ -290,7 +291,9 @@ def tile_list_biaff_silu_bias_kernel(
         ys = {}
         for step in range(CHUNKS + FINISH_LAG):
             if step < CHUNKS:
-                scale_round(nc.vector, ha, act_a, sa_bank, step)
+                split = (step + 1) * CHUNK - GPSIMD_COLS
+                scale_round(nc.vector, ha, act_a, sa_bank, step * CHUNK, split)
+                scale_round(nc.gpsimd, ha, act_a, sa_cols, split, (step + 1) * CHUNK)
             if 0 <= step - 1 < CHUNKS:
                 cols = slice((step - 1) * CHUNK, step * CHUNK)
                 quantize(ha[:, cols, :], ha_codes[:, cols], ha_sc[:, cols])

@@ -27,6 +27,7 @@ CHUNKS = M // CHUNK
 HALF = 256
 TAB_ROW = (8, 12)
 GPSIMD_COLS = 32
+EARLY_CHUNKS = 3
 FINISH_LAG = 3
 
 
@@ -55,7 +56,7 @@ def tile_list_biaff_silu_bias_kernel(
         vb_sc1 = held("vb_sc1", [P, J // 4], I32)
         tab_sc = placed("tab_sc", [P, T // 4], I32, 0)
         wb_sc_raw = placed("wb_sc_raw", [P, PASSES, R // 4], I32, 18432)
-        factor_rows = held("factor_rows", [P, P], F32)
+        factor_rows = held("factor_rows", [2, R], F32)
         ident = held("ident", [P, P], F32)
         tab2_w = held("tab2_w", [P, T], I32)
         wb_raw = held("wb_raw", [P, PASSES, R // 2], I32)
@@ -65,14 +66,14 @@ def tile_list_biaff_silu_bias_kernel(
         nc.gpsimd.memset(tab2_sc[:], 0)
         nc.gpsimd.memset(tab_sc[:], 0)
         nc.vector.memset(wb_sc_raw[:], 0)
-        nc.vector.memset(factor_rows[:], 0.0)
         nc.vector.memset(vb_sc1[:], 0)
 
+        warm = held("warm", [P, 2], F32)
+        nc.vector.memset(warm[:, 0:1], 0.0)
+        nc.scalar.activation(warm[:, 1:2], warm[:, 0:1], SILU)
+
         def load_factor(row, vec):
-            nc.sync.dma_start(
-                factor_rows[row : row + SLOTS, :].rearrange("t (g i) -> t g i", i=8),
-                vec.rearrange("(g t i) -> t g i", t=4, i=8),
-            )
+            nc.sync.dma_start(factor_rows[row : row + 1, :], vec.unsqueeze(0))
 
         ts = tab_scales.bitcast(I32).rearrange("a (q r) n -> q a r n", r=4)
         for q in range(4):
@@ -102,13 +103,13 @@ def tile_list_biaff_silu_bias_kernel(
         nc.sync.dma_start(vb_sc1[0 : P - 16, :], vb_sc0[16:P, :].bitcast(I32))
         vb_sc = [vb_sc0[:], vb_sc1[:].bitcast(U8)]
         load_factor(0, sb)
-        load_factor(SLOTS, sa)
+        load_factor(1, sa)
         wa_raw.append(placed("wa_raw1", [P, SLOTS, R], F32, 9216))
         nc.sync.dma_start(wa_raw[1][:], wa_rows(1))
 
         wb_codes = held("wb_codes", [P, PASSES, R // 2], I32)
         wb_sc = held("wb_sc", [P, PASSES, R // 4], I32)
-        vb_pairs = [held("vb_pairs0", [P, HALF], U32)]
+        vb_pairs = [placed("vb_pairs0", [P, HALF], U32, 27136)]
         vb_codes = [held("vb_codes%d" % h, [P, PASSES, 2 * HALF], U8) for h in range(2)]
 
         def gather_b(h):
@@ -128,11 +129,11 @@ def tile_list_biaff_silu_bias_kernel(
             wb_raw[:].rearrange("p a (g t w) -> p a t g w", t=4, w=4),
         )
         gather_b(0)
-        part_b(0)
         nc.vector.tensor_copy(
             wb_sc[:].rearrange("p a (t g w) -> p a t g w", t=4, w=2),
             wb_sc_raw[:].rearrange("p a (g t w) -> p a t g w", t=4, w=2),
         )
+        part_b(0)
         vb_pairs.append(placed("vb_pairs1", [P, HALF], U32, 18432))
         gather_b(1)
         tab_w.append(held("tab_w0", [P, T], I32, "tab2_w"))
@@ -142,7 +143,7 @@ def tile_list_biaff_silu_bias_kernel(
         load_tab(1)
         va_sc0 = placed("va_sc0", [P, M], U8, 18432)
         nc.vector.tensor_copy(va_sc0[:], tab_sc[:].bitcast(U8).indirect(list_a[:]))
-        b_all = held("b_all", [P, J], F32, "vb_pairs0")
+        b_all = placed("b_all", [P, J], F32, 27648)
         nc.sync.dma_start(b_all[:], b.partition_broadcast(P))
 
         def quantize(values, codes, scales):
@@ -169,17 +170,21 @@ def tile_list_biaff_silu_bias_kernel(
                 cast_wa(nc.scalar.copy, 0, t)
             else:
                 cast_wa_gpsimd(0, t)
+        factor_sorted = held("factor_sorted", [P, R], F32)
+        nc.vector.memset(factor_sorted[:], 0.0)
+        nc.vector.tensor_copy(
+            factor_sorted[0:2, :].rearrange("p (t g i) -> p t g i", t=4, i=8),
+            factor_rows[:].rearrange("p (g t i) -> p t g i", t=4, i=8),
+        )
 
-
-        hb = {}
         hb_sc = held("hb_sc", [P, J], U8)
         act_b = held("act_b", [P, 2, J, 2], F32)
-        for h in range(2):
-            cols = slice(h * HALF, (h + 1) * HALF)
-            zb = [bank(2 * h), bank(2 * h + 1)]
-            for a in range(PASSES):
+        zb = [bank(n) for n in range(4)]
+        for a in range(PASSES):
+            for h in range(2):
+                cols = slice(h * HALF, (h + 1) * HALF)
                 for t in range(SLOTS):
-                    z = zb[t // 2]
+                    z = zb[2 * h + t // 2]
                     nc.tensor.matmul_mx(
                         z[:, (t % 2) * HALF : (t % 2 + 1) * HALF],
                         lhsT=wb_codes[:, a, P // 2 * t : P // 2 * (t + 1)].bitcast(FP4X4),
@@ -192,17 +197,14 @@ def tile_list_biaff_silu_bias_kernel(
                     if a == PASSES - 1 and t % 2 == 1:
                         nc.scalar.activation(act_b[:, t // 2, cols, :], z[:].rearrange("p (e n) -> p n e", e=2), SILU)
 
-        factor_bank = bank(1)
-        nc.tensor.transpose(factor_bank[:, 0:P], factor_rows[:], ident[:])
-        sa_bank = factor_bank[:, SLOTS : 2 * SLOTS]
+        factor_bank = bank(7)
+        for t in range(SLOTS):
+            nc.tensor.transpose(factor_bank[:, 2 * t : 2 * t + P], factor_sorted[:, P * t : P * (t + 1)], ident[:])
+        sa_bank = factor_bank[:, 1 : 2 * SLOTS : 2]
         factor_cols = held("factor_cols", [P, 2 * SLOTS], F32)
-        nc.scalar.copy(factor_cols[:], factor_bank[:, 0 : 2 * SLOTS])
+        nc.scalar.copy(factor_cols[:].rearrange("p (v t) -> p v t", v=2), factor_bank[:, 0 : 2 * SLOTS].rearrange("p (t v) -> p v t", v=2))
         sb_cols = factor_cols[:, 0:SLOTS]
         sa_cols = factor_cols[:, SLOTS : 2 * SLOTS]
-
-        hb[0] = held("hb0", [P, HALF, SLOTS], BF16)
-        for t in range(SLOTS):
-            nc.scalar.activation(hb[0][:, :, t], act_b[:, t // 2, 0:HALF, t % 2], COPY, scale=sb_cols[:, t : t + 1])
 
         wa_codes = [placed("wa_codes0", [P, R], U32, 0), held("wa_codes1", [P, R], U32)]
         wa_sc = [held("wa_sc%d" % a, [P, R], U8) for a in range(PASSES)]
@@ -220,7 +222,7 @@ def tile_list_biaff_silu_bias_kernel(
                 tab_w[a][:].bitcast(U32).indirect(list_a[:, HALF // 16 * h : HALF // 16 * (h + 1)]),
             )
 
-        def sums_a(z, a, c):
+        def sums_a(z, a, c, first):
             cols = slice(c * CHUNK, (c + 1) * CHUNK)
             for t in range(SLOTS):
                 nc.tensor.matmul_mx(
@@ -229,29 +231,32 @@ def tile_list_biaff_silu_bias_kernel(
                     lhsT_scale=wa_sc[a][:, P * t : P * (t + 1)],
                     rhs=va_codes[a][:, cols].bitcast(FP8X4),
                     rhs_scale=va_sc0[TAB_ROW[a] : P, cols],
-                    start=(a == 0 and t == 0),
-                    stop=(a == PASSES - 1 and t == SLOTS - 1),
+                    start=(first and t == 0),
+                    stop=(not first and t == SLOTS - 1),
                 )
 
-        def scale_round_b(engine, factors, c):
+        def scale_round_b(engine, factors, lo, hi):
             engine.tensor_tensor(
-                hb[c // 2][:, (c % 2) * CHUNK : (c % 2 + 1) * CHUNK, :].rearrange("p n (u e) -> p n u e", e=2),
-                act_b[:, :, c * CHUNK : (c + 1) * CHUNK, :].rearrange("p u n e -> p n u e"),
-                factors[:, 0:SLOTS].rearrange("p (u e) -> p u e", e=2).unsqueeze(1).to_broadcast([P, CHUNK, 2, 2]),
+                hb[1][:, lo - HALF : hi - HALF, :].rearrange("p n (u e) -> p n u e", e=2),
+                act_b[:, :, lo:hi, :].rearrange("p u n e -> p n u e"),
+                factors[:, 0:SLOTS].rearrange("p (u e) -> p u e", e=2).unsqueeze(1).to_broadcast([P, hi - lo, 2, 2]),
                 MULT,
             )
 
         for t in range(SLOTS):
             cast_wa(nc.vector.tensor_copy, 1, t)
+        hb = [held("hb0", [P, HALF, SLOTS], BF16)]
+        for t in range(SLOTS):
+            nc.scalar.activation(hb[0][:, :, t], act_b[:, t // 2, 0:HALF, t % 2], COPY, scale=sb_cols[:, t : t + 1])
         quantize(wa_bf[1][:], wa_codes[1][:], wa_sc[1][:])
         gather_words(0, 0)
         gather_words(0, 1)
-        hb[1] = held("hb1", [P, HALF, SLOTS], BF16, "wa_bf1")
-        scale_round_b(nc.gpsimd, sb_cols, 2)
-        scale_round_b(nc.gpsimd, sb_cols, 3)
-        za = [bank(n) for n in (4, 5, 6, 7)]
-        for c in range(CHUNKS):
-            sums_a(za[c], 0, c)
+        hb.append(held("hb1", [P, HALF, SLOTS], BF16, "wa_bf1"))
+        scale_round_b(nc.gpsimd, sb_cols, HALF, HALF + CHUNK)
+        scale_round_b(nc.gpsimd, sb_cols, HALF + CHUNK, J)
+        za = [bank(n) for n in (4, 5, 6, 0)]
+        for c in range(EARLY_CHUNKS):
+            sums_a(za[c], 0, c, True)
 
         gather_words(1, 0)
         gather_words(1, 1)
@@ -260,7 +265,9 @@ def tile_list_biaff_silu_bias_kernel(
             quantize(hb[h][:], hb_codes[:, h * HALF : (h + 1) * HALF], hb_sc[:, h * HALF : (h + 1) * HALF])
         act_a = held("act_a", [P, M, SLOTS], F32)
         for c in range(CHUNKS):
-            sums_a(za[c], 1, c)
+            sums_a(za[c], 1, c, c >= EARLY_CHUNKS)
+            if c >= EARLY_CHUNKS:
+                sums_a(za[c], 0, c, False)
             nc.scalar.activation(
                 act_a[:, c * CHUNK : (c + 1) * CHUNK, :], za[c][:].rearrange("p (t n) -> p n t", t=SLOTS), SILU
             )
@@ -271,7 +278,7 @@ def tile_list_biaff_silu_bias_kernel(
 
         def score(c):
             cols = slice(c * CHUNK, (c + 1) * CHUNK)
-            y = bank((0, 2, 3, 4)[c])
+            y = bank(c + 1)
             nc.tensor.matmul_mx(
                 y[:],
                 lhsT=ha_codes[:, cols].bitcast(FP8X4),

@@ -139,12 +139,8 @@ def tile_list_biaff_silu_bias_kernel(
         tab_w.append(held("tab_w0", [P, T], I32, "tab2_w"))
         load_tab(0)
         part_b(1)
-        tab_w.append(placed("tab_w1", [P, T], I32, 18944))
-        load_tab(1)
         va_sc0 = placed("va_sc0", [P, M], U8, 18432)
         nc.vector.tensor_copy(va_sc0[:], tab_sc[:].bitcast(U8).indirect(list_a[:]))
-        b_all = placed("b_all", [P, J], F32, 27648)
-        nc.sync.dma_start(b_all[:], b.partition_broadcast(P))
 
         def quantize(values, codes, scales):
             nc.vector.quantize_mx(
@@ -153,7 +149,7 @@ def tile_list_biaff_silu_bias_kernel(
                 in_=values.rearrange("p n t -> p (n t)"),
             )
 
-        wa_bf = [held("wa_bf%d" % a, [P, R, SLOTS], BF16) for a in range(PASSES)]
+        wa_bf = [placed("wa_bf0", [P, R, SLOTS], BF16, 20480), held("wa_bf1", [P, R, SLOTS], BF16)]
 
         def cast_wa(copy, a, t):
             src = wa_raw[a][:].rearrange("p j (g t u i) -> p t g u j i", t=4, u=2, i=4)
@@ -210,6 +206,8 @@ def tile_list_biaff_silu_bias_kernel(
         wa_sc = [held("wa_sc%d" % a, [P, R], U8) for a in range(PASSES)]
         va_codes = [held("va_codes%d" % a, [P, M], U32) for a in range(PASSES)]
         quantize(wa_bf[0][:], wa_codes[0][:], wa_sc[0][:])
+        tab_w.append(placed("tab_w1", [P, T], I32, 18944))
+        load_tab(1)
 
         def scale_round(engine, dst, act, factors, lo, hi):
             engine.tensor_tensor(
@@ -251,6 +249,8 @@ def tile_list_biaff_silu_bias_kernel(
         quantize(wa_bf[1][:], wa_codes[1][:], wa_sc[1][:])
         gather_words(0, 0)
         gather_words(0, 1)
+        b_all = held("b_all", [P, J], F32, "tab2_w")
+        nc.sync.dma_start(b_all[:], b.partition_broadcast(P))
         hb.append(held("hb1", [P, HALF, SLOTS], BF16, "wa_bf1"))
         scale_round_b(nc.gpsimd, sb_cols, HALF, HALF + CHUNK)
         scale_round_b(nc.gpsimd, sb_cols, HALF + CHUNK, J)

@@ -58,7 +58,7 @@ def tile_list_biaff_silu_bias_kernel(
         wb_sc_raw = placed("wb_sc_raw", [P, PASSES, R // 4], I32, 18432)
         factor_rows = held("factor_rows", [2, R], F32)
         ident = held("ident", [P, P], F32)
-        tab2_w = held("tab2_w", [P, T], I32)
+        tab2_w = placed("tab2_w", [P, T], I32, 57344)
         wb_raw = held("wb_raw", [P, PASSES, R // 2], I32)
         wa_raw = [held("wa_raw0", [P, SLOTS, R], F32)]
         tab_w = []
@@ -136,7 +136,7 @@ def tile_list_biaff_silu_bias_kernel(
         part_b(0)
         vb_pairs.append(placed("vb_pairs1", [P, HALF], U32, 18432))
         gather_b(1)
-        tab_w.append(held("tab_w0", [P, T], I32, "tab2_w"))
+        tab_w.append(placed("tab_w0", [P, T], I32, 57344))
         load_tab(0)
         part_b(1)
         va_sc0 = placed("va_sc0", [P, M], U8, 18432)
@@ -202,7 +202,7 @@ def tile_list_biaff_silu_bias_kernel(
         sb_cols = factor_cols[:, 0:SLOTS]
         sa_cols = factor_cols[:, SLOTS : 2 * SLOTS]
 
-        wa_codes = [placed("wa_codes0", [P, R], U32, 0), held("wa_codes1", [P, R], U32)]
+        wa_codes = [placed("wa_codes0", [P, R], U32, 0)]
         wa_sc = [held("wa_sc%d" % a, [P, R], U8) for a in range(PASSES)]
         va_codes = [held("va_codes%d" % a, [P, M], U32) for a in range(PASSES)]
         quantize(wa_bf[0][:], wa_codes[0][:], wa_sc[0][:])
@@ -233,27 +233,29 @@ def tile_list_biaff_silu_bias_kernel(
                     stop=(not first and t == SLOTS - 1),
                 )
 
-        def scale_round_b(engine, factors, lo, hi):
-            engine.tensor_tensor(
-                hb[1][:, lo - HALF : hi - HALF, :].rearrange("p n (u e) -> p n u e", e=2),
-                act_b[:, :, lo:hi, :].rearrange("p u n e -> p n u e"),
-                factors[:, 0:SLOTS].rearrange("p (u e) -> p u e", e=2).unsqueeze(1).to_broadcast([P, hi - lo, 2, 2]),
+        def times_sb_gpsimd(dst, c):
+            nc.gpsimd.tensor_tensor(
+                dst[:].rearrange("p n (u e) -> p n u e", e=2),
+                act_b[:, :, c * CHUNK : (c + 1) * CHUNK, :].rearrange("p u n e -> p n u e"),
+                sb_cols.rearrange("p (u e) -> p u e", e=2).unsqueeze(1).to_broadcast([P, CHUNK, 2, 2]),
                 MULT,
             )
 
         for t in range(SLOTS):
             cast_wa(nc.vector.tensor_copy, 1, t)
-        hb = [held("hb0", [P, HALF, SLOTS], BF16)]
+        hb_scalar = held("hb_scalar", [P, HALF, SLOTS], BF16)
         for t in range(SLOTS):
-            nc.scalar.activation(hb[0][:, :, t], act_b[:, t // 2, 0:HALF, t % 2], COPY, scale=sb_cols[:, t : t + 1])
-        quantize(wa_bf[1][:], wa_codes[1][:], wa_sc[1][:])
+            nc.scalar.activation(hb_scalar[:, :, t], act_b[:, t // 2, 0:HALF, t % 2], COPY, scale=sb_cols[:, t : t + 1])
+        hb_third = placed("hb_third", [P, CHUNK, SLOTS], BF16, 9216)
+        times_sb_gpsimd(hb_third, 2)
         gather_words(0, 0)
         gather_words(0, 1)
-        b_all = held("b_all", [P, J], F32, "tab2_w")
+        b_all = placed("b_all", [P, J], F32, 59392)
         nc.sync.dma_start(b_all[:], b.partition_broadcast(P))
-        hb.append(held("hb1", [P, HALF, SLOTS], BF16, "wa_bf1"))
-        scale_round_b(nc.gpsimd, sb_cols, HALF, HALF + CHUNK)
-        scale_round_b(nc.gpsimd, sb_cols, HALF + CHUNK, J)
+        wa_codes.append(placed("wa_codes1", [P, R], U32, 57344))
+        quantize(wa_bf[1][:], wa_codes[1][:], wa_sc[1][:])
+        hb_fourth = held("hb_fourth", [P, CHUNK, SLOTS], BF16, "wa_bf1")
+        times_sb_gpsimd(hb_fourth, 3)
         za = [bank(n) for n in (4, 5, 6, 0)]
         for c in range(EARLY_CHUNKS):
             sums_a(za[c], 0, c, True)
@@ -261,8 +263,8 @@ def tile_list_biaff_silu_bias_kernel(
         gather_words(1, 0)
         gather_words(1, 1)
         hb_codes = placed("hb_codes", [P, J], U32, 18944)
-        for h in range(2):
-            quantize(hb[h][:], hb_codes[:, h * HALF : (h + 1) * HALF], hb_sc[:, h * HALF : (h + 1) * HALF])
+        for values, lo, hi in ((hb_third, HALF, HALF + CHUNK), (hb_scalar, 0, HALF), (hb_fourth, HALF + CHUNK, J)):
+            quantize(values[:], hb_codes[:, lo:hi], hb_sc[:, lo:hi])
         act_a = held("act_a", [P, M, SLOTS], F32)
         for c in range(CHUNKS):
             sums_a(za[c], 1, c, c >= EARLY_CHUNKS)

from contextlib import ExitStack

import concourse.mybir as mybir
from concourse.masks import make_identity

K, R, T, M, J = 1024, 512, 2048, 512, 512
FLOPS = 2 * K * R * M + 2 * K * R * J + 2 * R * M * J

F32 = mybir.dt.float32
BF16 = mybir.dt.bfloat16
I32 = mybir.dt.int32
U32 = mybir.dt.uint32
U16 = mybir.dt.uint16
U8 = mybir.dt.uint8
FP8X4 = mybir.dt.float8_e4m3fn_x4
FP4X4 = mybir.dt.float4_e2m1fn_x4
MULT = mybir.AluOpType.mult
ADD = mybir.AluOpType.add
SILU = mybir.ActivationFunctionType.Silu
COPY = mybir.ActivationFunctionType.Copy

P = 128
PASSES = K // 512
SLOTS = 4
CHUNK = 128
CHUNKS = M // CHUNK
HALF = 256
TAB_ROW = (8, 12)
GPSIMD_COLS = 32
EARLY_CHUNKS = 3
FINISH_LAG = 3


def tile_list_biaff_silu_bias_kernel(
    tc, tab_words, tab_scales, tab2_words, tab2_scales, wa, wb_words, wb_scales, sa, sb, b, offs, offs2, out
):
    nc = tc.nc
    with ExitStack() as ctx:
        keep = ctx.enter_context(tc.tile_pool(name="keep", bufs=1))
        laid = ctx.enter_context(tc.tile_pool(name="laid", bufs=1))
        ring = ctx.enter_context(tc.tile_pool(name="ring", bufs=CHUNKS))
        psum = ctx.enter_context(tc.psum_pool(name="psum", bufs=1))

        def bank(n):
            return psum.tile([P, 512], F32, name="bank%d" % n, tag="bank%d" % n)

        def held(name, shape, dtype, slot=None):
            return keep.tile(shape, dtype, name=name, tag=slot or name, align_bytes=64)

        def placed(name, shape, dtype, offset):
            return laid.tile(shape, dtype, name=name, offset=offset, align_bytes=64)

        list_a = keep.tile([P, M // 16], U16, name="list_a")
        list_b = keep.tile([P, J // 16], U16, name="list_b")
        tab2_sc = placed("tab2_sc", [P, T // 4], I32, 8192)
        vb_sc1 = held("vb_sc1", [P, J // 4], I32)
        tab_sc = placed("tab_sc", [P, T // 4], I32, 0)
        wb_sc_raw = placed("wb_sc_raw", [P, PASSES, R // 4], I32, 18432)
        factor_rows = held("factor_rows", [2, R], F32)
        ident = held("ident", [P, P], F32)
        tab2_w = placed("tab2_w", [P, T], I32, 57344)
        wb_raw = held("wb_raw", [P, PASSES, R // 2], I32)
        wa_raw = [held("wa_raw0", [P, SLOTS, R], F32)]
        tab_w = []

        nc.gpsimd.memset(tab2_sc[:], 0)
        nc.gpsimd.memset(tab_sc[:], 0)
        nc.vector.memset(wb_sc_raw[:], 0)
        nc.vector.memset(vb_sc1[:], 0)

        warm = held("warm", [P, 2], F32)
        nc.vector.memset(warm[:, 0:1], 0.0)
        nc.scalar.activation(warm[:, 1:2], warm[:, 0:1], SILU)

        def load_factor(row, vec):
            nc.sync.dma_start(factor_rows[row : row + 1, :], vec.unsqueeze(0))

        ts = tab_scales.bitcast(I32).rearrange("a (q r) n -> q a r n", r=4)
        for q in range(4):
            nc.gpsimd.dma_start(tab_sc[32 * q + TAB_ROW[0] : 32 * q + TAB_ROW[0] + 8, :], ts[q])
        make_identity(nc, ident[:])

        nc.sync.dma_start(wb_raw[:], wb_words.bitcast(I32).rearrange("a p n -> p a n"))
        nc.sync.dma_start(list_b[:], offs2)
        nc.sync.dma_start(list_a[:], offs)
        t2s = tab2_scales.bitcast(I32).rearrange("a (q r) n -> r q a n", r=4)
        for r in range(4):
            nc.sync.dma_start(tab2_sc[r:P:16, :], t2s[r])
        nc.sync.dma_start(tab2_w[:], tab2_words[0].rearrange("p t i -> p (t i)").bitcast(I32))
        wbs = wb_scales.bitcast(I32).rearrange("a (q r) n -> r q a n", r=4)
        for r in range(4):
            nc.sync.dma_start(wb_sc_raw[r:P:32, :, :], wbs[r])

        def wa_rows(a):
            return wa[512 * a : 512 * (a + 1), :].rearrange("(p j) r -> p j r", j=4)

        def load_tab(a):
            nc.sync.dma_start(tab_w[a][:], tab_words[a].rearrange("p t i -> p (t i)").bitcast(I32))

        nc.sync.dma_start(wa_raw[0][:], wa_rows(0))
        vb_sc0 = held("vb_sc0", [P, J], U8)
        nc.vector.tensor_copy(vb_sc0[:], tab2_sc[:].bitcast(U8).indirect(list_b[:]))
        nc.sync.dma_start(vb_sc1[0 : P - 16, :], vb_sc0[16:P, :].bitcast(I32))
        vb_sc = [vb_sc0[:], vb_sc1[:].bitcast(U8)]
        load_factor(0, sb)
        load_factor(1, sa)
        wa_raw.append(placed("wa_raw1", [P, SLOTS, R], F32, 9216))
        nc.sync.dma_start(wa_raw[1][:], wa_rows(1))

        wb_codes = held("wb_codes", [P, PASSES, R // 2], I32)
        wb_sc = held("wb_sc", [P, PASSES, R // 4], I32)
        vb_pairs = [placed("vb_pairs0", [P, HALF], U32, 27136)]
        vb_codes = [held("vb_codes%d" % h, [P, PASSES, 2 * HALF], U8) for h in range(2)]

        def gather_b(h):
            nc.vector.tensor_copy(
                vb_pairs[h][:],
                tab2_w[:].bitcast(U32).indirect(list_b[:, HALF // 16 * h : HALF // 16 * (h + 1)]),
            )

        def part_b(h):
            nc.vector.tensor_copy(
                vb_codes[h][:].rearrange("p a n -> p (a n)").bitcast(U16).rearrange("p (a j) -> p a j", a=2),
                vb_pairs[h][:].bitcast(U16).rearrange("p (j a) -> p a j", a=2),
            )

        nc.vector.tensor_copy(
            wb_codes[:].rearrange("p a (t g w) -> p a t g w", t=4, w=4),
            wb_raw[:].rearrange("p a (g t w) -> p a t g w", t=4, w=4),
        )
        gather_b(0)
        nc.vector.tensor_copy(
            wb_sc[:].rearrange("p a (t g w) -> p a t g w", t=4, w=2),
            wb_sc_raw[:].rearrange("p a (g t w) -> p a t g w", t=4, w=2),
        )
        part_b(0)
        vb_pairs.append(placed("vb_pairs1", [P, HALF], U32, 18432))
        gather_b(1)
        tab_w.append(placed("tab_w0", [P, T], I32, 57344))
        load_tab(0)
        part_b(1)
        va_sc0 = placed("va_sc0", [P, M], U8, 18432)
        nc.vector.tensor_copy(va_sc0[:], tab_sc[:].bitcast(U8).indirect(list_a[:]))

        def quantize(values, codes, scales):
            nc.vector.quantize_mx(
                out=codes.bitcast(FP8X4),
                scales=scales,
                in_=values.rearrange("p n t -> p (n t)"),
            )

        wa_bf = [placed("wa_bf0", [P, R, SLOTS], BF16, 20480), held("wa_bf1", [P, R, SLOTS], BF16)]

        def cast_wa(copy, a, t):
            src = wa_raw[a][:].rearrange("p j (g t u i) -> p t g u j i", t=4, u=2, i=4)
            dst = wa_bf[a][:].rearrange("p (t g u i) j -> p t g u j i", t=4, u=2, i=4)
            copy(dst[:, t], src[:, t])

        def cast_wa_gpsimd(a, t):
            src = wa_raw[a][:].rearrange("p j (g t i) -> p t g i j", t=4, i=8)
            dst = wa_bf[a][:].rearrange("p (t g i) j -> p t g i j", t=4, i=8)
            nc.gpsimd.tensor_scalar(dst[:, t], src[:, t], 1.0, 0.0, MULT, ADD)

        for t in range(SLOTS):
            if t < 2:
                cast_wa(nc.scalar.copy, 0, t)
            else:
                cast_wa_gpsimd(0, t)
        factor_sorted = held("factor_sorted", [P, R], F32)
        nc.vector.memset(factor_sorted[:], 0.0)
        nc.vector.tensor_copy(
            factor_sorted[0:2, :].rearrange("p (t g i) -> p t g i", t=4, i=8),
            factor_rows[:].rearrange("p (g t i) -> p t g i", t=4, i=8),
        )

        hb_sc = held("hb_sc", [P, J], U8)
        act_b = held("act_b", [P, 2, J, 2], F32)
        zb = [bank(n) for n in range(4)]
        for a in range(PASSES):
            for h in range(2):
                cols = slice(h * HALF, (h + 1) * HALF)
                for t in range(SLOTS):
                    z = zb[2 * h + t // 2]
                    nc.tensor.matmul_mx(
                        z[:, (t % 2) * HALF : (t % 2 + 1) * HALF],
                        lhsT=wb_codes[:, a, P // 2 * t : P // 2 * (t + 1)].bitcast(FP4X4),
                        lhsT_scale=wb_sc[:, a, P // 4 * t : P // 4 * (t + 1)].bitcast(U8),
                        rhs=vb_codes[h][:, a, :].bitcast(FP4X4),
                        rhs_scale=vb_sc[a][:, cols],
                        start=(a == 0 and t % 2 == 0),
                        stop=(a == PASSES - 1 and t % 2 == 1),
                    )
                    if a == PASSES - 1 and t % 2 == 1:
                        nc.scalar.activation(act_b[:, t // 2, cols, :], z[:].rearrange("p (e n) -> p n e", e=2), SILU)

        factor_bank = bank(7)
        for t in range(SLOTS):
            nc.tensor.transpose(factor_bank[:, 2 * t : 2 * t + P], factor_sorted[:, P * t : P * (t + 1)], ident[:])
        sa_bank = factor_bank[:, 1 : 2 * SLOTS : 2]
        factor_cols = held("factor_cols", [P, 2 * SLOTS], F32)
        nc.scalar.copy(factor_cols[:].rearrange("p (v t) -> p v t", v=2), factor_bank[:, 0 : 2 * SLOTS].rearrange("p (t v) -> p v t", v=2))
        sb_cols = factor_cols[:, 0:SLOTS]
        sa_cols = factor_cols[:, SLOTS : 2 * SLOTS]

        wa_codes = [placed("wa_codes0", [P, R], U32, 0)]
        wa_sc = [held("wa_sc%d" % a, [P, R], U8) for a in range(PASSES)]
        va_codes = [held("va_codes%d" % a, [P, M], U32) for a in range(PASSES)]
        quantize(wa_bf[0][:], wa_codes[0][:], wa_sc[0][:])
        tab_w.append(placed("tab_w1", [P, T], I32, 18944))
        load_tab(1)

        def scale_round(engine, dst, act, factors, lo, hi):
            engine.tensor_tensor(
                dst[:, lo:hi, :], act[:, lo:hi, :], factors[:, 0:SLOTS].unsqueeze(1).to_broadcast([P, hi - lo, SLOTS]), MULT
            )

        def gather_words(a, h):
            nc.vector.tensor_copy(
                va_codes[a][:, h * HALF : (h + 1) * HALF],
                tab_w[a][:].bitcast(U32).indirect(list_a[:, HALF // 16 * h : HALF // 16 * (h + 1)]),
            )

        def sums_a(z, a, c, first):
            cols = slice(c * CHUNK, (c + 1) * CHUNK)
            for t in range(SLOTS):
                nc.tensor.matmul_mx(
                    z[:, t * CHUNK : (t + 1) * CHUNK],
                    lhsT=wa_codes[a][:, P * t : P * (t + 1)].bitcast(FP8X4),
                    lhsT_scale=wa_sc[a][:, P * t : P * (t + 1)],
                    rhs=va_codes[a][:, cols].bitcast(FP8X4),
                    rhs_scale=va_sc0[TAB_ROW[a] : P, cols],
                    start=(first and t == 0),
                    stop=(not first and t == SLOTS - 1),
                )

        def times_sb_gpsimd(dst, c):
            nc.gpsimd.tensor_tensor(
                dst[:].rearrange("p n (u e) -> p n u e", e=2),
                act_b[:, :, c * CHUNK : (c + 1) * CHUNK, :].rearrange("p u n e -> p n u e"),
                sb_cols.rearrange("p (u e) -> p u e", e=2).unsqueeze(1).to_broadcast([P, CHUNK, 2, 2]),
                MULT,
            )

        for t in range(SLOTS):
            cast_wa(nc.vector.tensor_copy, 1, t)
        hb_scalar = held("hb_scalar", [P, HALF, SLOTS], BF16)
        for t in range(SLOTS):
            nc.scalar.activation(hb_scalar[:, :, t], act_b[:, t // 2, 0:HALF, t % 2], COPY, scale=sb_cols[:, t : t + 1])
        hb_third = placed("hb_third", [P, CHUNK, SLOTS], BF16, 9216)
        times_sb_gpsimd(hb_third, 2)
        gather_words(0, 0)
        gather_words(0, 1)
        b_all = placed("b_all", [P, J], F32, 59392)
        nc.sync.dma_start(b_all[:], b.partition_broadcast(P))
        wa_codes.append(placed("wa_codes1", [P, R], U32, 57344))
        quantize(wa_bf[1][:], wa_codes[1][:], wa_sc[1][:])
        hb_fourth = held("hb_fourth", [P, CHUNK, SLOTS], BF16, "wa_bf1")
        times_sb_gpsimd(hb_fourth, 3)
        za = [bank(n) for n in (4, 5, 6, 0)]
        for c in range(EARLY_CHUNKS):
            sums_a(za[c], 0, c, True)

        gather_words(1, 0)
        gather_words(1, 1)
        hb_codes = placed("hb_codes", [P, J], U32, 18944)
        for values, lo, hi in ((hb_third, HALF, HALF + CHUNK), (hb_scalar, 0, HALF), (hb_fourth, HALF + CHUNK, J)):
            quantize(values[:], hb_codes[:, lo:hi], hb_sc[:, lo:hi])
        act_a = held("act_a", [P, M, SLOTS], F32)
        for c in range(CHUNKS):
            sums_a(za[c], 1, c, c >= EARLY_CHUNKS)
            if c >= EARLY_CHUNKS:
                sums_a(za[c], 0, c, False)
            nc.scalar.activation(
                act_a[:, c * CHUNK : (c + 1) * CHUNK, :], za[c][:].rearrange("p (t n) -> p n t", t=SLOTS), SILU
            )

        ha = held("ha", [P, M, SLOTS], BF16)
        ha_codes = held("ha_codes", [P, M], U32)
        ha_sc = held("ha_sc", [P, M], U8)

        def score(c):
            cols = slice(c * CHUNK, (c + 1) * CHUNK)
            y = bank(c + 1)
            nc.tensor.matmul_mx(
                y[:],
                lhsT=ha_codes[:, cols].bitcast(FP8X4),
                lhsT_scale=ha_sc[:, cols],
                rhs=hb_codes[:].bitcast(FP8X4),
                rhs_scale=hb_sc[:],
                start=True,
                stop=True,
            )
            return y

        def finish(c, y):
            res = ring.tile([P, J], F32, name="res")
            nc.vector.scalar_tensor_tensor(res[:], y[:], 0.03125, b_all[:], MULT, ADD)
            nc.sync.dma_start(out[c * CHUNK : (c + 1) * CHUNK, :], res[:])

        ys = {}
        for step in range(CHUNKS + FINISH_LAG):
            if step < CHUNKS:
                split = (step + 1) * CHUNK - GPSIMD_COLS
                scale_round(nc.vector, ha, act_a, sa_bank, step * CHUNK, split)
                scale_round(nc.gpsimd, ha, act_a, sa_cols, split, (step + 1) * CHUNK)
            if 0 <= step - 1 < CHUNKS:
                cols = slice((step - 1) * CHUNK, step * CHUNK)
                quantize(ha[:, cols, :], ha_codes[:, cols], ha_sc[:, cols])
                ys[step - 1] = score(step - 1)
            if step >= FINISH_LAG:
                finish(step - FINISH_LAG, ys[step - FINISH_LAG])
